import numpy as np
import ml_dtypes


def mxq(x, axis, fmt="e4m3"):
    dtype, down = {"e4m3": (ml_dtypes.float8_e4m3fn, 7), "e5m2": (ml_dtypes.float8_e5m2, 14)}[fmt]
    v = np.moveaxis(np.asarray(x, np.float32).astype(ml_dtypes.bfloat16).astype(np.float64), axis, -1)
    blocks = v.reshape(v.shape[:-1] + (-1, 32))
    amax = np.abs(blocks).max(-1, keepdims=True)
    byte = np.maximum(np.where(amax > 0, np.frexp(amax)[1] - 1 + 127, 0) - down, 1)
    scale = np.exp2(byte - 127.0)
    codes = (blocks / scale).astype(np.float32).astype(dtype).astype(np.float64)
    return np.moveaxis((codes * scale).reshape(v.shape), -1, axis)


WIDE = False


def mx_kscale(k):
    if not WIDE:
        return np.ones(k)
    levels = np.array([10, -10, 5, -5, 0])
    if k % 512:
        return np.exp2(np.random.permutation(np.resize(levels, k // 32))).repeat(32)
    a = np.empty((k // 512, 16))
    for p in range(k // 512):
        a[p, :8] = np.random.permutation(np.resize(levels, 8))
        for g in range(8):
            far = levels[np.abs(levels - a[p, g]) >= 10]
            a[p, g + 8] = far[np.random.randint(len(far))]
    return np.exp2(a.ravel()).repeat(32)


def f64(x):
    return np.asarray(x).astype(np.float64)


def striped(idx):
    return np.tile(idx.reshape(-1, 16).T, (8, 1)).astype(np.uint16)


def unstriped(offs):
    return offs[:16].T.reshape(-1).astype(np.int64)


E2M1 = np.array([0.0, 0.5, 1.0, 1.5, 2.0, 3.0, 4.0, 6.0, -0.0, -0.5, -1.0, -1.5, -2.0, -3.0, -4.0, -6.0])


def pack_weight(w, fmt):
    k, n = w.shape
    w = f64(np.asarray(w, np.float32).astype(ml_dtypes.bfloat16)).reshape(k // 32, 32, n)
    amax = np.abs(w).max(1)
    if fmt == "e4m3":
        byte = np.frexp(amax)[1] - 1 + 127 - 7
    else:
        mant, ex = np.frexp(amax / 6.0)
        byte = np.where(mant > 0.5, ex, ex - 1) + 127
    byte = np.clip(np.where(amax > 0, byte, 1), 1, 254)
    scaled = (w * np.exp2(127.0 - byte)[:, None, :]).reshape(k, n).astype(np.float32)
    by_word = np.ascontiguousarray(scaled.reshape(k // 512, 128, 4, n).transpose(0, 1, 3, 2))
    if fmt == "e4m3":
        words = by_word.astype(ml_dtypes.float8_e4m3fn).view(np.uint8)
    else:
        c = by_word.astype(ml_dtypes.float4_e2m1fn).view(np.uint8) & 0xF
        words = (c[..., 0::2] | (c[..., 1::2] << 4)).reshape(k // 512, 128, 2 * n)
    return np.ascontiguousarray(words), np.ascontiguousarray(byte.astype(np.uint8).reshape(k // 512, 16, n))


def unpack_weight(words, scales, fmt):
    g, _, n = scales.shape
    words = np.ascontiguousarray(words).reshape(g, 128, n, -1)
    if fmt == "e4m3":
        vals = words.view(ml_dtypes.float8_e4m3fn).astype(np.float64)
    else:
        nib = np.empty((g, 128, n, 4), np.uint8)
        nib[..., 0::2] = words & 0xF
        nib[..., 1::2] = words >> 4
        vals = E2M1[nib]
    vals = vals * np.repeat(np.exp2(scales.astype(np.float64) - 127.0), 8, axis=1)[..., None]
    return vals.transpose(0, 1, 3, 2).reshape(g * 512, n)


def gelu(v):
    return 0.5 * v * (1.0 + np.tanh(np.sqrt(2.0 / np.pi) * (v + 0.044715 * v**3)))


K, H, N, T, S = 1024, 512, 256, 2048, 1024

def setup_inputs():
    n = np.random.standard_normal
    s = mx_kscale(K)[:, None]
    u = mx_kscale(H)[:, None]
    tab_words, tab_scales = pack_weight(n((K, T)) * s, "e4m3")
    wb_words, wb_scales = pack_weight(n((K, H)) / np.sqrt(K) / s, "e2m1")
    return {
        "tab_words": tab_words, "tab_scales": tab_scales,
        "offs": striped(np.random.permutation(T)[:S]),
        "gT": n((N, T)).astype(np.float32),
        "wa": (n((K, H)) / np.sqrt(K) / s).astype(np.float32),
        "wb_words": wb_words, "wb_scales": wb_scales,
        "hw": (np.exp(0.3 * n(H)) * u[:, 0]).astype(np.float32),
        "wo": (n((H, N)) / np.sqrt(H) / u).astype(np.float32),
    }

def reference(tab_words, tab_scales, offs, gT, wa, wb_words, wb_scales, hw, wo):
    v = unpack_weight(tab_words, tab_scales, "e4m3")[:, unstriped(offs)]
    g = f64(gT)[:, unstriped(offs)]
    wb = unpack_weight(wb_words, wb_scales, "e2m1")
    A = mxq(f64(wa), 0, "e4m3").T @ v
    B = wb.T @ v
    h = f64(hw)[:, None] * (A * A - B)
    y = mxq(f64(wo), 0, "e4m3").T @ mxq(h, 0, "e4m3")
    return 0.5 * y + g

@@ -1,0 +1,288 @@
+from contextlib import ExitStack
+
+import concourse.mybir as mybir
+from concourse.masks import make_identity
+
+K, H, N, T, S = 1024, 512, 256, 2048, 1024
+FLOPS = 2 * K * H * S * 2 + 2 * H * N * S
+
+F32 = mybir.dt.float32
+BF16 = mybir.dt.bfloat16
+I32 = mybir.dt.int32
+U32 = mybir.dt.uint32
+U16 = mybir.dt.uint16
+U8 = mybir.dt.uint8
+FP8X4 = mybir.dt.float8_e4m3fn_x4
+FP4X4 = mybir.dt.float4_e2m1fn_x4
+ALU = mybir.AluOpType
+AX = mybir.AxisListType
+ACT = mybir.ActivationFunctionType
+
+P = 128
+PACK = 4
+PASSES = K // (P * PACK)
+HALF = 512
+QUART = 256
+
+
+def tile_list_campaign_interaction_logits_kernel(
+    tc, tab_words, tab_scales, offs, gT, wa, wb_words, wb_scales, hw, wo, out
+):
+    nc = tc.nc
+    with ExitStack() as ctx:
+        keep = ctx.enter_context(tc.tile_pool(name="keep", bufs=1))
+        stage = ctx.enter_context(tc.tile_pool(name="stage", bufs=1))
+        psum = ctx.enter_context(tc.psum_pool(name="psum", bufs=8))
+
+        def sb(name, shape, dtype):
+            return keep.tile(shape, dtype, name=name, align_bytes=64)
+
+        offsets = keep.tile([P, S // 16], U16, name="offsets")
+        nc.sync.dma_start(offsets[:], offs)
+
+        def staged(name, shape, dtype, tag):
+            return stage.tile(shape, dtype, name=name, tag=tag, align_bytes=64)
+
+        wb_sc_raw = sb("wb_sc_raw", [P, PASSES, H // 4], I32)
+        nc.gpsimd.memset(wb_sc_raw[:], 0)
+        v_sc1 = sb("v_sc1", [P, S // 4], I32)
+        nc.vector.memset(v_sc1[:], 0)
+
+        hw_blk = sb("hw_blk", [P, PACK, 8], F32)
+        nc.gpsimd.dma_start(
+            hw_blk[:].rearrange("p t i -> p (t i)"),
+            hw.rearrange("(g c) -> g c", c=32).unsqueeze(1).broadcast_to([16, 8, 32]),
+        )
+        ident = sb("ident", [P, P], F32)
+        make_identity(nc, ident[:])
+        own = sb("own", [P, 8], F32)
+        nc.vector.tensor_reduce(own[:], ident[:].rearrange("p (g i) -> p i g", i=8), AX.X, ALU.add)
+        hw_m = sb("hw_m", [P, PACK, 8], F32)
+        nc.gpsimd.tensor_tensor(hw_m[:], hw_blk[:], own[:].unsqueeze(1).broadcast_to([P, PACK, 8]), ALU.mult)
+        hw_4 = sb("hw_4", [P, PACK, 4], F32)
+        nc.gpsimd.tensor_tensor(hw_4[:], hw_m[:, :, 0:4], hw_m[:, :, 4:8], ALU.add)
+        hw_2 = sb("hw_2", [P, PACK, 2], F32)
+        nc.gpsimd.tensor_tensor(hw_2[:], hw_4[:, :, 0:2], hw_4[:, :, 2:4], ALU.add)
+        hw_1 = sb("hw_1", [P, PACK], F32)
+        nc.gpsimd.tensor_tensor(hw_1[:], hw_2[:, :, 0], hw_2[:, :, 1], ALU.add)
+        hw_t = hw_1[:]
+
+        tab_sc = staged("tab_sc", [P, T // 4], I32, "a")
+        tab_rows = tab_scales.bitcast(I32).rearrange("a r c -> (a r) c")
+        nc.sync.dma_start(tab_sc[0:32, :], tab_rows)
+        for q in range(1, 4):
+            nc.sync.dma_start(
+                tab_sc[32 * q : 32 * q + 32, :],
+                tab_rows[4 * q : 4 * q + 4, :].unsqueeze(0).broadcast_to([8, 4, T // 4]),
+            )
+        tab_w = [staged(f"tab_w{a}", [P, T], I32, "bc"[a]) for a in range(PASSES)]
+        nc.sync.dma_start(tab_w[0][:], tab_words[0].rearrange("p t i -> p (t i)").bitcast(I32))
+        wb_raw = sb("wb_raw", [P, PASSES, H // 2], I32)
+        nc.sync.dma_start(wb_raw[:], wb_words.bitcast(I32).rearrange("a p c -> p a c"))
+        wb_sc_hbm = wb_scales.bitcast(I32).rearrange("a r c -> r a c")
+        for q in range(4):
+            nc.sync.dma_start(wb_sc_raw[32 * q : 32 * q + 4, :, :], wb_sc_hbm[4 * q : 4 * q + 4])
+        nc.sync.dma_start(tab_w[1][:], tab_words[1].rearrange("p t i -> p (t i)").bitcast(I32))
+
+        rs = sb("rs", [P, PACK], F32)
+        nc.scalar.activation(rs[:], hw_t, ACT.Abs_reciprocal_sqrt)
+        root0 = sb("root0", [P, PACK], F32)
+        nc.gpsimd.tensor_tensor(root0[:], hw_t, rs[:], ALU.mult)
+        prod = sb("prod", [P, PACK], F32)
+        nc.gpsimd.tensor_tensor(prod[:], root0[:], rs[:], ALU.mult)
+        corr = sb("corr", [P, PACK], F32)
+        nc.gpsimd.tensor_scalar(corr[:], prod[:], -0.5, 1.5, ALU.mult, ALU.add)
+        root = sb("root", [P, PACK], F32)
+        nc.gpsimd.tensor_tensor(root[:], root0[:], corr[:], ALU.mult)
+
+        v_sc = sb("v_sc", [P, S], U8)
+        nc.vector.tensor_copy(v_sc[:], tab_sc[:].bitcast(U8).indirect(offsets[:]))
+        for q in range(4):
+            nc.sync.dma_start(v_sc1[32 * q : 32 * q + 4, :], v_sc[16 + 4 * q : 20 + 4 * q, :].bitcast(I32))
+
+        def load_wa(a):
+            raw = staged(f"wa_raw{a}", [P, PACK, H], F32, "ab"[a])
+            nc.sync.dma_start(
+                raw[:], wa[a * P * PACK : (a + 1) * P * PACK, :].rearrange("(p j) c -> p j c", j=PACK)
+            )
+            return raw
+
+        def load_g(u):
+            rows = staged(f"g_tab{u}", [P, T], F32, "cb"[u])
+            nc.sync.dma_start(rows[:], gT[u * P : (u + 1) * P, :])
+            return rows
+
+        wa_raw = [load_wa(0)]
+
+        v0 = sb("v0", [P, S], U32)
+        nc.vector.tensor_copy(v0[:], tab_w[0][:].bitcast(U32).indirect(offsets[:]))
+        wa_raw.append(load_wa(1))
+
+        wb_sc = sb("wb_sc", [P, PACK, PASSES, P // 4], I32)
+        nc.vector.tensor_copy(
+            wb_sc[:].rearrange("p t a (g w) -> p t (a g) w", w=2),
+            wb_sc_raw[:].rearrange("p a (g t w) -> p t (a g) w", t=PACK, w=2),
+        )
+        wb_w = sb("wb_w", [P, PACK, PASSES, P // 2], I32)
+        nc.vector.tensor_copy(
+            wb_w[:].rearrange("p t a (g w) -> p t (a g) w", w=4),
+            wb_raw[:].rearrange("p a (g t w) -> p t (a g) w", t=PACK, w=4),
+        )
+
+        v1 = [sb(f"v1_{c}", [P, HALF], U32) for c in range(2)]
+        for c in range(2):
+            nc.vector.tensor_copy(v1[c][:], tab_w[1][:].bitcast(U32).indirect(offsets[:, 32 * c : 32 * (c + 1)]))
+        g_tab = [load_g(0)]
+
+        def v_codes(a, c):
+            return (v0[:, c * HALF : (c + 1) * HALF] if a == 0 else v1[c][:]).bitcast(FP8X4)
+
+        banks_b = {}
+        for a in range(PASSES):
+            for c in range(2):
+                cols = slice(c * HALF, (c + 1) * HALF)
+                for t in range(PACK):
+                    if a == 0:
+                        banks_b[c, t] = psum.tile([P, HALF], F32, name="bank", tag="bank")
+                    nc.tensor.matmul_mx(
+                        out=banks_b[c, t][:],
+                        lhsT=wb_w[:, t, a, :].bitcast(FP4X4),
+                        lhsT_scale=wb_sc[:, t, a, :].bitcast(U8),
+                        rhs=v_codes(a, c),
+                        rhs_scale=v_sc[:, cols] if a == 0 else v_sc1[:].bitcast(U8)[:, cols],
+                        start=(a == 0),
+                        stop=(a == PASSES - 1),
+                    )
+        hb = [sb(f"hb{c}", [P, PACK, HALF], F32) for c in range(2)]
+        for c in range(2):
+            for t in range(PACK):
+                nc.scalar.activation(hb[c][:, t, :], banks_b[c, t][:], ACT.Copy, scale=hw_1[:, t : t + 1])
+
+        wa_bf = {}
+        wa_w = {}
+        wa_sc = {}
+
+        def wa_round(a, t):
+            wa_bf[a, t] = sb(f"wa_bf{a}{t}", [P, P, PACK], BF16)
+            nc.vector.tensor_copy(
+                wa_bf[a, t][:].rearrange("p (g i) j -> p g i j", i=8),
+                wa_raw[a][:].rearrange("p j (g t i) -> p t g i j", t=PACK, i=8)[:, t],
+            )
+
+        def wa_quant(a, t):
+            wa_w[a, t] = sb(f"wa_w{a}{t}", [P, P], U32)
+            wa_sc[a, t] = sb(f"wa_sc{a}{t}", [P, P], U8)
+            nc.vector.quantize_mx(
+                out=wa_w[a, t][:].bitcast(FP8X4),
+                scales=wa_sc[a, t][:],
+                in_=wa_bf[a, t][:].rearrange("p m j -> p (m j)"),
+            )
+
+        steps = [(a, t) for a in range(PASSES) for t in range(PACK)]
+        for s in range(len(steps) + 1):
+            if s < len(steps):
+                wa_round(*steps[s])
+            if s > 0:
+                wa_quant(*steps[s - 1])
+            if s == PACK - 1:
+                wo_raw = staged("wo_raw", [P, PACK, N], F32, "a")
+                wo_hbm = wo.rearrange("(g t i) n -> t g i n", t=PACK, i=8)
+                for t in range(PACK):
+                    nc.sync.dma_start(wo_raw[:, t, :], wo_hbm[t])
+        g_tab.append(load_g(1))
+
+        banks_a = {}
+        for c in range(2):
+            for a in range(PASSES):
+                cols = slice(c * HALF, (c + 1) * HALF)
+                for t in range(PACK):
+                    if a == 0:
+                        banks_a[c, t] = psum.tile([P, HALF], F32, name="bank", tag="bank")
+                    nc.tensor.matmul_mx(
+                        out=banks_a[c, t][:],
+                        lhsT=wa_w[a, t][:].bitcast(FP8X4),
+                        lhsT_scale=wa_sc[a, t][:],
+                        rhs=v_codes(a, c),
+                        rhs_scale=v_sc[:, cols] if a == 0 else v_sc1[:].bitcast(U8)[:, cols],
+                        start=(a == 0),
+                        stop=(a == PASSES - 1),
+                    )
+
+        g_pick = sb("g_pick", [P, 2, S], F32)
+        nc.vector.tensor_copy(g_pick[:, 0, :], g_tab[0][:].indirect(offsets[:]))
+
+        sq = [sb(f"sq{q}", [P, PACK, QUART], F32) for q in range(4)]
+
+        def squares(q):
+            c, lo = q // 2, (q % 2) * QUART
+            for t in range(PACK):
+                nc.scalar.activation(
+                    sq[q][:, t, :], banks_a[c, t][:, lo : lo + QUART], ACT.Square, scale=root[:, t : t + 1]
+                )
+
+        for q in range(4):
+            squares(q)
+        wo_bf = sb("wo_bf", [P, N, PACK], BF16)
+        nc.gpsimd.tensor_scalar(
+            wo_bf[:].rearrange("p (c i) t -> p c t i", i=4),
+            wo_raw[:].rearrange("p t (c i) -> p c t i", i=4),
+            1.0,
+            0.0,
+            ALU.mult,
+            ALU.add,
+        )
+
+        h_bf = [sb(f"h_bf{q}", [P, QUART, PACK], BF16) for q in range(4)]
+        h_w = [sb(f"h_w{q}", [P, QUART], U32) for q in range(4)]
+        h_sc = [sb(f"h_sc{q}", [P, QUART], U8) for q in range(4)]
+        res = [sb(f"res{q}", [P, 2, QUART], F32) for q in range(4)]
+        wo_w = sb("wo_w", [P, N], U32)
+        wo_sc = sb("wo_sc", [P, N], U8)
+        out_v = out.rearrange("(u p) j -> p u j", p=P)
+
+        def subtract(q):
+            c, lo = q // 2, (q % 2) * QUART
+            nc.vector.tensor_tensor(
+                h_bf[q][:].rearrange("p (c i) t -> p c t i", i=4),
+                sq[q][:].rearrange("p t (c i) -> p c t i", i=4),
+                hb[c][:, :, lo : lo + QUART].rearrange("p t (c i) -> p c t i", i=4),
+                ALU.subtract,
+            )
+
+        def quant_h(q):
+            nc.vector.quantize_mx(
+                out=h_w[q][:].bitcast(FP8X4), scales=h_sc[q][:], in_=h_bf[q][:].rearrange("p j t -> p (j t)")
+            )
+
+        def finish(q):
+            cols = slice(q * QUART, (q + 1) * QUART)
+            y = psum.tile([P, 2, QUART], F32, name="bank", tag="bank")
+            for u in range(2):
+                nc.tensor.matmul_mx(
+                    out=y[:, u, :],
+                    lhsT=wo_w[:, u * P : (u + 1) * P].bitcast(FP8X4),
+                    lhsT_scale=wo_sc[:, u * P : (u + 1) * P],
+                    rhs=h_w[q][:].bitcast(FP8X4),
+                    rhs_scale=h_sc[q][:],
+                    start=True,
+                    stop=True,
+                )
+            nc.vector.scalar_tensor_tensor(res[q][:], y[:], 0.5, g_pick[:, :, cols], ALU.mult, ALU.add)
+            nc.sync.dma_start(out_v[:, :, cols], res[q][:])
+
+        subtract(0)
+        nc.vector.quantize_mx(
+            out=wo_w[:].bitcast(FP8X4), scales=wo_sc[:], in_=wo_bf[:].rearrange("p n t -> p (n t)")
+        )
+        quant_h(0)
+        nc.vector.tensor_copy(g_pick[:, 1, :], g_tab[1][:].indirect(offsets[:]))
+        subtract(1)
+        finish(0)
+        quant_h(1)
+        subtract(2)
+        quant_h(2)
+        subtract(3)
+        finish(1)
+        quant_h(3)
+        finish(2)
+        finish(3)

@@ -15,7 +15,6 @@ U8 = mybir.dt.uint8
 FP8X4 = mybir.dt.float8_e4m3fn_x4
 FP4X4 = mybir.dt.float4_e2m1fn_x4
 ALU = mybir.AluOpType
-AX = mybir.AxisListType
 ACT = mybir.ActivationFunctionType
 
 P = 128
@@ -32,7 +31,7 @@ def tile_list_campaign_interaction_logits_kernel(
     with ExitStack() as ctx:
         keep = ctx.enter_context(tc.tile_pool(name="keep", bufs=1))
         stage = ctx.enter_context(tc.tile_pool(name="stage", bufs=1))
-        psum = ctx.enter_context(tc.psum_pool(name="psum", bufs=8))
+        psum = ctx.enter_context(tc.psum_pool(name="psum", bufs=1))
 
         def sb(name, shape, dtype):
             return keep.tile(shape, dtype, name=name, align_bytes=64)
@@ -43,30 +42,13 @@ def tile_list_campaign_interaction_logits_kernel(
         def staged(name, shape, dtype, tag):
             return stage.tile(shape, dtype, name=name, tag=tag, align_bytes=64)
 
-        wb_sc_raw = sb("wb_sc_raw", [P, PASSES, H // 4], I32)
-        nc.gpsimd.memset(wb_sc_raw[:], 0)
+        wb_sc_raw = staged("wb_sc_raw", [P, PASSES, H // 4], I32, "d")
+        wb_sc = sb("wb_sc", [P, PACK, PASSES, P // 4], I32)
+        nc.vector.memset(wb_sc[:], 0)
         v_sc1 = sb("v_sc1", [P, S // 4], I32)
         nc.vector.memset(v_sc1[:], 0)
 
         hw_blk = sb("hw_blk", [P, PACK, 8], F32)
-        nc.gpsimd.dma_start(
-            hw_blk[:].rearrange("p t i -> p (t i)"),
-            hw.rearrange("(g c) -> g c", c=32).unsqueeze(1).broadcast_to([16, 8, 32]),
-        )
-        ident = sb("ident", [P, P], F32)
-        make_identity(nc, ident[:])
-        own = sb("own", [P, 8], F32)
-        nc.vector.tensor_reduce(own[:], ident[:].rearrange("p (g i) -> p i g", i=8), AX.X, ALU.add)
-        hw_m = sb("hw_m", [P, PACK, 8], F32)
-        nc.gpsimd.tensor_tensor(hw_m[:], hw_blk[:], own[:].unsqueeze(1).broadcast_to([P, PACK, 8]), ALU.mult)
-        hw_4 = sb("hw_4", [P, PACK, 4], F32)
-        nc.gpsimd.tensor_tensor(hw_4[:], hw_m[:, :, 0:4], hw_m[:, :, 4:8], ALU.add)
-        hw_2 = sb("hw_2", [P, PACK, 2], F32)
-        nc.gpsimd.tensor_tensor(hw_2[:], hw_4[:, :, 0:2], hw_4[:, :, 2:4], ALU.add)
-        hw_1 = sb("hw_1", [P, PACK], F32)
-        nc.gpsimd.tensor_tensor(hw_1[:], hw_2[:, :, 0], hw_2[:, :, 1], ALU.add)
-        hw_t = hw_1[:]
-
         tab_sc = staged("tab_sc", [P, T // 4], I32, "a")
         tab_rows = tab_scales.bitcast(I32).rearrange("a r c -> (a r) c")
         nc.sync.dma_start(tab_sc[0:32, :], tab_rows)
@@ -76,13 +58,32 @@ def tile_list_campaign_interaction_logits_kernel(
                 tab_rows[4 * q : 4 * q + 4, :].unsqueeze(0).broadcast_to([8, 4, T // 4]),
             )
         tab_w = [staged(f"tab_w{a}", [P, T], I32, "bc"[a]) for a in range(PASSES)]
-        nc.sync.dma_start(tab_w[0][:], tab_words[0].rearrange("p t i -> p (t i)").bitcast(I32))
-        wb_raw = sb("wb_raw", [P, PASSES, H // 2], I32)
+        nc.sync.dma_start(
+            hw_blk[:].rearrange("p t i -> p (t i)"),
+            hw.rearrange("(g c) -> g c", c=32).unsqueeze(1).broadcast_to([16, 8, 32]),
+        )
+        wb_raw = staged("wb_raw", [P, PASSES, H // 2], I32, "f")
         nc.sync.dma_start(wb_raw[:], wb_words.bitcast(I32).rearrange("a p c -> p a c"))
+        nc.sync.dma_start(tab_w[0][:], tab_words[0].rearrange("p t i -> p (t i)").bitcast(I32))
         wb_sc_hbm = wb_scales.bitcast(I32).rearrange("a r c -> r a c")
         for q in range(4):
             nc.sync.dma_start(wb_sc_raw[32 * q : 32 * q + 4, :, :], wb_sc_hbm[4 * q : 4 * q + 4])
         nc.sync.dma_start(tab_w[1][:], tab_words[1].rearrange("p t i -> p (t i)").bitcast(I32))
+
+        def fold(name, src, width):
+            while src.shape[-1] > width:
+                half = src.shape[-1] // 2
+                dst = sb(f"{name}{half}", [P, src.shape[1], half], F32)
+                nc.gpsimd.tensor_tensor(dst[:], src[:, :, 0:half], src[:, :, half : 2 * half], ALU.add)
+                src = dst[:]
+            return src
+
+        ident = sb("ident", [P, 1, P], F32)
+        make_identity(nc, ident[:, 0, :])
+        own = fold("own", ident[:], 8)
+        hw_m = sb("hw_m", [P, PACK, 8], F32)
+        nc.gpsimd.tensor_tensor(hw_m[:], hw_blk[:], own.broadcast_to([P, PACK, 8]), ALU.mult)
+        hw_t = fold("hw", hw_m[:], 1)[:, :, 0]
 
         rs = sb("rs", [P, PACK], F32)
         nc.scalar.activation(rs[:], hw_t, ACT.Abs_reciprocal_sqrt)
@@ -100,139 +101,147 @@ def tile_list_campaign_interaction_logits_kernel(
         for q in range(4):
             nc.sync.dma_start(v_sc1[32 * q : 32 * q + 4, :], v_sc[16 + 4 * q : 20 + 4 * q, :].bitcast(I32))
 
-        def load_wa(a):
-            raw = staged(f"wa_raw{a}", [P, PACK, H], F32, "ab"[a])
-            nc.sync.dma_start(
-                raw[:], wa[a * P * PACK : (a + 1) * P * PACK, :].rearrange("(p j) c -> p j c", j=PACK)
-            )
-            return raw
-
         def load_g(u):
-            rows = staged(f"g_tab{u}", [P, T], F32, "cb"[u])
+            rows = staged(f"g_tab{u}", [P, T], F32, "bc"[u])
             nc.sync.dma_start(rows[:], gT[u * P : (u + 1) * P, :])
             return rows
 
-        wa_raw = [load_wa(0)]
+        v = {}
 
-        v0 = sb("v0", [P, S], U32)
-        nc.vector.tensor_copy(v0[:], tab_w[0][:].bitcast(U32).indirect(offsets[:]))
-        wa_raw.append(load_wa(1))
+        def gather_words(a, c, dst):
+            v[a, c] = dst
+            nc.vector.tensor_copy(dst, tab_w[a][:].bitcast(U32).indirect(offsets[:, 32 * c : 32 * (c + 1)]))
 
-        wb_sc = sb("wb_sc", [P, PACK, PASSES, P // 4], I32)
-        nc.vector.tensor_copy(
-            wb_sc[:].rearrange("p t a (g w) -> p t (a g) w", w=2),
-            wb_sc_raw[:].rearrange("p a (g t w) -> p t (a g) w", t=PACK, w=2),
-        )
-        wb_w = sb("wb_w", [P, PACK, PASSES, P // 2], I32)
+        wb_w = staged("wb_w", [P, PACK, PASSES, P // 2], I32, "a")
         nc.vector.tensor_copy(
             wb_w[:].rearrange("p t a (g w) -> p t (a g) w", w=4),
             wb_raw[:].rearrange("p a (g t w) -> p t (a g) w", t=PACK, w=4),
         )
-
-        v1 = [sb(f"v1_{c}", [P, HALF], U32) for c in range(2)]
-        for c in range(2):
-            nc.vector.tensor_copy(v1[c][:], tab_w[1][:].bitcast(U32).indirect(offsets[:, 32 * c : 32 * (c + 1)]))
-        g_tab = [load_g(0)]
-
-        def v_codes(a, c):
-            return (v0[:, c * HALF : (c + 1) * HALF] if a == 0 else v1[c][:]).bitcast(FP8X4)
-
-        banks_b = {}
+        wa_raw = staged("wa_raw", [P, PASSES, PACK, H], F32, "f")
         for a in range(PASSES):
-            for c in range(2):
-                cols = slice(c * HALF, (c + 1) * HALF)
-                for t in range(PACK):
-                    if a == 0:
-                        banks_b[c, t] = psum.tile([P, HALF], F32, name="bank", tag="bank")
-                    nc.tensor.matmul_mx(
-                        out=banks_b[c, t][:],
-                        lhsT=wb_w[:, t, a, :].bitcast(FP4X4),
-                        lhsT_scale=wb_sc[:, t, a, :].bitcast(U8),
-                        rhs=v_codes(a, c),
-                        rhs_scale=v_sc[:, cols] if a == 0 else v_sc1[:].bitcast(U8)[:, cols],
-                        start=(a == 0),
-                        stop=(a == PASSES - 1),
-                    )
-        hb = [sb(f"hb{c}", [P, PACK, HALF], F32) for c in range(2)]
-        for c in range(2):
-            for t in range(PACK):
-                nc.scalar.activation(hb[c][:, t, :], banks_b[c, t][:], ACT.Copy, scale=hw_1[:, t : t + 1])
-
-        wa_bf = {}
-        wa_w = {}
-        wa_sc = {}
-
-        def wa_round(a, t):
-            wa_bf[a, t] = sb(f"wa_bf{a}{t}", [P, P, PACK], BF16)
+            nc.sync.dma_start(
+                wa_raw[:, a], wa[a * P * PACK : (a + 1) * P * PACK, :].rearrange("(p j) c -> p j c", j=PACK)
+            )
+        gather_words(0, 0, sb("v00", [P, HALF], U32)[:])
+        for q in range(4):
+            rows = slice(32 * q, 32 * q + 4)
             nc.vector.tensor_copy(
-                wa_bf[a, t][:].rearrange("p (g i) j -> p g i j", i=8),
-                wa_raw[a][:].rearrange("p j (g t i) -> p t g i j", t=PACK, i=8)[:, t],
+                wb_sc[rows].rearrange("p t a (g w) -> p t (a g) w", w=2),
+                wb_sc_raw[rows].rearrange("p a (g t w) -> p t (a g) w", t=PACK, w=2),
             )
-
-        def wa_quant(a, t):
-            wa_w[a, t] = sb(f"wa_w{a}{t}", [P, P], U32)
-            wa_sc[a, t] = sb(f"wa_sc{a}{t}", [P, P], U8)
-            nc.vector.quantize_mx(
-                out=wa_w[a, t][:].bitcast(FP8X4),
-                scales=wa_sc[a, t][:],
-                in_=wa_bf[a, t][:].rearrange("p m j -> p (m j)"),
-            )
-
-        steps = [(a, t) for a in range(PASSES) for t in range(PACK)]
-        for s in range(len(steps) + 1):
-            if s < len(steps):
-                wa_round(*steps[s])
-            if s > 0:
-                wa_quant(*steps[s - 1])
-            if s == PACK - 1:
-                wo_raw = staged("wo_raw", [P, PACK, N], F32, "a")
-                wo_hbm = wo.rearrange("(g t i) n -> t g i n", t=PACK, i=8)
-                for t in range(PACK):
-                    nc.sync.dma_start(wo_raw[:, t, :], wo_hbm[t])
+        v_mid = staged("v_mid", [P, 2, HALF], U32, "d")
+        gather_words(1, 0, v_mid[:, 0, :])
+        gather_words(0, 1, v_mid[:, 1, :])
+        g_tab = [load_g(0)]
+        gather_words(1, 1, sb("v11", [P, HALF], U32)[:])
         g_tab.append(load_g(1))
 
+        banks_b = {}
+
+        def product_b(c):
+            cols = slice(c * HALF, (c + 1) * HALF)
+            for t, a in [(t, a) for t in range(PACK) for a in range(PASSES)]:
+                if a == 0:
+                    banks_b[c, t] = psum.tile([P, HALF], F32, name=f"b{c}{t}", tag=f"bank{t}")
+                nc.tensor.matmul_mx(
+                    out=banks_b[c, t][:],
+                    lhsT=wb_w[:, t, a, :].bitcast(FP4X4),
+                    lhsT_scale=wb_sc[:, t, a, :].bitcast(U8),
+                    rhs=v[a, c].bitcast(FP8X4),
+                    rhs_scale=v_sc[:, cols] if a == 0 else v_sc1[:].bitcast(U8)[:, cols],
+                    start=(a == 0),
+                    stop=(a == PASSES - 1),
+                )
+
+        hb = [sb(f"hb{c}", [P, PACK, HALF], F32) for c in range(2)]
+
+        def weigh_b(c):
+            for t in range(PACK):
+                nc.scalar.activation(hb[c][:, t, :], banks_b[c, t][:], ACT.Copy, scale=hw_t[:, t : t + 1])
+
+        product_b(0)
+        weigh_b(0)
+        product_b(1)
+        weigh_b(1)
+
+        wa_w = {}
+        wa_sc = {}
+        pieces = [(0, 0, 2), (0, 2, 4), (1, 0, 2), (1, 2, 4)]
+        wa_bf = {}
+        for a, lo, hi in pieces:
+            if (a, lo) == (0, 0):
+                wa_bf[a, lo] = staged(f"wa_bf{a}{lo}", [P, hi - lo, P, PACK], BF16, "g")
+            else:
+                wa_bf[a, lo] = sb(f"wa_bf{a}{lo}", [P, hi - lo, P, PACK], BF16)
+
+        def wa_round(a, lo, hi, t0, t1):
+            nc.vector.tensor_copy(
+                wa_bf[a, lo][:, t0 - lo : t1 - lo].rearrange("p t (g i) j -> p t g i j", i=8),
+                wa_raw[:, a].rearrange("p j (g t i) -> p t g i j", t=PACK, i=8)[:, t0:t1],
+            )
+
+        def wa_quant(a, lo, hi):
+            codes = sb(f"wa_w{a}{lo}", [P, hi - lo, P], U32)
+            scales = sb(f"wa_sc{a}{lo}", [P, hi - lo, P], U8)
+            nc.vector.quantize_mx(
+                out=codes[:].rearrange("p t m -> p (t m)").bitcast(FP8X4),
+                scales=scales[:].rearrange("p t m -> p (t m)"),
+                in_=wa_bf[a, lo][:].rearrange("p t m j -> p (t m j)"),
+            )
+            for t in range(lo, hi):
+                wa_w[a, t] = codes[:, t - lo, :]
+                wa_sc[a, t] = scales[:, t - lo, :]
+
+        wa_round(0, 0, 2, 0, 2)
+        wa_round(0, 2, 4, 2, 4)
+        wa_quant(0, 0, 2)
+        wo_raw = staged("wo_raw", [P, PACK, N], F32, "g")
+        wo_hbm = wo.rearrange("(g t i) n -> t g i n", t=PACK, i=8)
+        for t in range(PACK):
+            nc.sync.dma_start(wo_raw[:, t, :], wo_hbm[t])
+        wa_round(1, 0, 2, 0, 2)
+        wa_quant(0, 2, 4)
+        wa_quant(1, 0, 2)
+        wa_round(1, 2, 4, 2, 4)
+        g_pick = sb("g_pick", [P, 2, S], F32)
+        wa_quant(1, 2, 4)
+
         banks_a = {}
-        for c in range(2):
-            for a in range(PASSES):
-                cols = slice(c * HALF, (c + 1) * HALF)
-                for t in range(PACK):
-                    if a == 0:
-                        banks_a[c, t] = psum.tile([P, HALF], F32, name="bank", tag="bank")
+
+        def product_a(q):
+            c, lo = q // 2, (q % 2) * QUART
+            cols = slice(q * QUART, (q + 1) * QUART)
+            for t in range(PACK):
+                if t % 2 == 0:
+                    bank = psum.tile([P, 2, QUART], F32, name=f"a{q}{t}", tag=f"bank{(4 + 2 * q + t // 2) % 8}")
+                banks_a[q, t] = bank[:, t % 2, :]
+                for a in range(PASSES):
                     nc.tensor.matmul_mx(
-                        out=banks_a[c, t][:],
-                        lhsT=wa_w[a, t][:].bitcast(FP8X4),
-                        lhsT_scale=wa_sc[a, t][:],
-                        rhs=v_codes(a, c),
+                        out=banks_a[q, t],
+                        lhsT=wa_w[a, t].bitcast(FP8X4),
+                        lhsT_scale=wa_sc[a, t],
+                        rhs=v[a, c][:, lo : lo + QUART].bitcast(FP8X4),
                         rhs_scale=v_sc[:, cols] if a == 0 else v_sc1[:].bitcast(U8)[:, cols],
                         start=(a == 0),
                         stop=(a == PASSES - 1),
                     )
 
-        g_pick = sb("g_pick", [P, 2, S], F32)
+        product_a(0)
         nc.vector.tensor_copy(g_pick[:, 0, :], g_tab[0][:].indirect(offsets[:]))
 
-        sq = [sb(f"sq{q}", [P, PACK, QUART], F32) for q in range(4)]
+        sq = {}
 
         def squares(q):
-            c, lo = q // 2, (q % 2) * QUART
+            sq[q] = sb(f"sq{q}", [P, PACK, QUART], F32)
             for t in range(PACK):
-                nc.scalar.activation(
-                    sq[q][:, t, :], banks_a[c, t][:, lo : lo + QUART], ACT.Square, scale=root[:, t : t + 1]
-                )
+                nc.scalar.activation(sq[q][:, t, :], banks_a[q, t], ACT.Square, scale=root[:, t : t + 1])
 
-        for q in range(4):
+        squares(0)
+        for q in range(1, 4):
+            product_a(q)
             squares(q)
-        wo_bf = sb("wo_bf", [P, N, PACK], BF16)
-        nc.gpsimd.tensor_scalar(
-            wo_bf[:].rearrange("p (c i) t -> p c t i", i=4),
-            wo_raw[:].rearrange("p t (c i) -> p c t i", i=4),
-            1.0,
-            0.0,
-            ALU.mult,
-            ALU.add,
-        )
 
-        h_bf = [sb(f"h_bf{q}", [P, QUART, PACK], BF16) for q in range(4)]
+        h_bf = {q: sb(f"h_bf{q}", [P, QUART, PACK], BF16) for q in range(2)}
         h_w = [sb(f"h_w{q}", [P, QUART], U32) for q in range(4)]
         h_sc = [sb(f"h_sc{q}", [P, QUART], U8) for q in range(4)]
         res = [sb(f"res{q}", [P, 2, QUART], F32) for q in range(4)]
@@ -240,14 +249,24 @@ def tile_list_campaign_interaction_logits_kernel(
         wo_sc = sb("wo_sc", [P, N], U8)
         out_v = out.rearrange("(u p) j -> p u j", p=P)
 
-        def subtract(q):
+        def subtract(q, j0=0):
             c, lo = q // 2, (q % 2) * QUART
             nc.vector.tensor_tensor(
-                h_bf[q][:].rearrange("p (c i) t -> p c t i", i=4),
-                sq[q][:].rearrange("p t (c i) -> p c t i", i=4),
-                hb[c][:, :, lo : lo + QUART].rearrange("p t (c i) -> p c t i", i=4),
+                h_bf[q][:, j0:, :].rearrange("p (c i) t -> p c t i", i=4),
+                sq[q][:, :, j0:].rearrange("p t (c i) -> p c t i", i=4),
+                hb[c][:, :, lo + j0 : lo + QUART].rearrange("p t (c i) -> p c t i", i=4),
                 ALU.subtract,
             )
+
+        def subtract_gpsimd(q, j1):
+            c, lo = q // 2, (q % 2) * QUART
+            for j in range(0, j1, P):
+                nc.gpsimd.tensor_tensor(
+                    h_bf[q][:, j : j + P, :],
+                    sq[q][:, :, j : j + P].rearrange("p t j -> p j t"),
+                    hb[c][:, :, lo + j : lo + j + P].rearrange("p t j -> p j t"),
+                    ALU.subtract,
+                )
 
         def quant_h(q):
             nc.vector.quantize_mx(
@@ -256,7 +275,7 @@ def tile_list_campaign_interaction_logits_kernel(
 
         def finish(q):
             cols = slice(q * QUART, (q + 1) * QUART)
-            y = psum.tile([P, 2, QUART], F32, name="bank", tag="bank")
+            y = psum.tile([P, 2, QUART], F32, name=f"y{q}", tag=f"bank{4 + q}")
             for u in range(2):
                 nc.tensor.matmul_mx(
                     out=y[:, u, :],
@@ -270,19 +289,27 @@ def tile_list_campaign_interaction_logits_kernel(
             nc.vector.scalar_tensor_tensor(res[q][:], y[:], 0.5, g_pick[:, :, cols], ALU.mult, ALU.add)
             nc.sync.dma_start(out_v[:, :, cols], res[q][:])
 
-        subtract(0)
+        nc.vector.tensor_copy(g_pick[:, 1, :], g_tab[1][:].indirect(offsets[:]))
+        subtract_gpsimd(0, QUART)
+        subtract_gpsimd(1, P)
+        wo_bf = staged("wo_bf", [P, N, PACK], BF16, "e")
+        nc.vector.tensor_copy(
+            wo_bf[:].rearrange("p (c i) t -> p c t i", i=4),
+            wo_raw[:].rearrange("p t (c i) -> p c t i", i=4),
+        )
+        quant_h(0)
         nc.vector.quantize_mx(
             out=wo_w[:].bitcast(FP8X4), scales=wo_sc[:], in_=wo_bf[:].rearrange("p n t -> p (n t)")
         )
-        quant_h(0)
-        nc.vector.tensor_copy(g_pick[:, 1, :], g_tab[1][:].indirect(offsets[:]))
-        subtract(1)
-        finish(0)
-        quant_h(1)
+        subtract(1, P)
+        h_bf[2] = staged("h_bf2", [P, QUART, PACK], BF16, "g")
         subtract(2)
+        quant_h(1)
         quant_h(2)
+        h_bf[3] = staged("h_bf3", [P, QUART, PACK], BF16, "e")
         subtract(3)
-        finish(1)
+        finish(0)
         quant_h(3)
+        finish(1)
         finish(2)
         finish(3)

@@ -1,7 +1,6 @@
 from contextlib import ExitStack
 
 import concourse.mybir as mybir
-from concourse.masks import make_identity
 
 K, H, N, T, S = 1024, 512, 256, 2048, 1024
 FLOPS = 2 * K * H * S * 2 + 2 * H * N * S
@@ -48,7 +47,12 @@ def tile_list_campaign_interaction_logits_kernel(
         v_sc1 = sb("v_sc1", [P, S // 4], I32)
         nc.vector.memset(v_sc1[:], 0)
 
-        hw_blk = sb("hw_blk", [P, PACK, 8], F32)
+        hw_pad = sb("hw_pad", [P, PACK, 8], F32)
+        hw_hbm = hw.rearrange("(g t i o) -> t g i o", t=PACK, i=8, o=1)
+        with nc.allow_non_contiguous_dma(reason="one channel weight per partition and slot"):
+            for t in range(PACK):
+                nc.gpsimd.dma_start(hw_pad[:, t, 0:1], hw_hbm[t])
+        hw_t = hw_pad[:, :, 0]
         tab_sc = staged("tab_sc", [P, T // 4], I32, "a")
         tab_rows = tab_scales.bitcast(I32).rearrange("a r c -> (a r) c")
         nc.sync.dma_start(tab_sc[0:32, :], tab_rows)
@@ -58,10 +62,6 @@ def tile_list_campaign_interaction_logits_kernel(
                 tab_rows[4 * q : 4 * q + 4, :].unsqueeze(0).broadcast_to([8, 4, T // 4]),
             )
         tab_w = [staged(f"tab_w{a}", [P, T], I32, "bc"[a]) for a in range(PASSES)]
-        nc.sync.dma_start(
-            hw_blk[:].rearrange("p t i -> p (t i)"),
-            hw.rearrange("(g c) -> g c", c=32).unsqueeze(1).broadcast_to([16, 8, 32]),
-        )
         wb_raw = staged("wb_raw", [P, PASSES, H // 2], I32, "f")
         nc.sync.dma_start(wb_raw[:], wb_words.bitcast(I32).rearrange("a p c -> p a c"))
         nc.sync.dma_start(tab_w[0][:], tab_words[0].rearrange("p t i -> p (t i)").bitcast(I32))
@@ -70,31 +70,20 @@ def tile_list_campaign_interaction_logits_kernel(
             nc.sync.dma_start(wb_sc_raw[32 * q : 32 * q + 4, :, :], wb_sc_hbm[4 * q : 4 * q + 4])
         nc.sync.dma_start(tab_w[1][:], tab_words[1].rearrange("p t i -> p (t i)").bitcast(I32))
 
-        def fold(name, src, width):
-            while src.shape[-1] > width:
-                half = src.shape[-1] // 2
-                dst = sb(f"{name}{half}", [P, src.shape[1], half], F32)
-                nc.gpsimd.tensor_tensor(dst[:], src[:, :, 0:half], src[:, :, half : 2 * half], ALU.add)
-                src = dst[:]
-            return src
-
-        ident = sb("ident", [P, 1, P], F32)
-        make_identity(nc, ident[:, 0, :])
-        own = fold("own", ident[:], 8)
-        hw_m = sb("hw_m", [P, PACK, 8], F32)
-        nc.gpsimd.tensor_tensor(hw_m[:], hw_blk[:], own.broadcast_to([P, PACK, 8]), ALU.mult)
-        hw_t = fold("hw", hw_m[:], 1)[:, :, 0]
-
         rs = sb("rs", [P, PACK], F32)
         nc.scalar.activation(rs[:], hw_t, ACT.Abs_reciprocal_sqrt)
-        root0 = sb("root0", [P, PACK], F32)
-        nc.gpsimd.tensor_tensor(root0[:], hw_t, rs[:], ALU.mult)
-        prod = sb("prod", [P, PACK], F32)
-        nc.gpsimd.tensor_tensor(prod[:], root0[:], rs[:], ALU.mult)
+
+        def times(name, x, y):
+            prod = sb(name, [P, PACK], F32)
+            for t in range(PACK):
+                nc.scalar.activation(prod[:, t : t + 1], x[:, t : t + 1], ACT.Copy, scale=y[:, t : t + 1])
+            return prod
+
+        root0 = times("root0", hw_t, rs)
+        near_one = times("near_one", root0, rs)
         corr = sb("corr", [P, PACK], F32)
-        nc.gpsimd.tensor_scalar(corr[:], prod[:], -0.5, 1.5, ALU.mult, ALU.add)
-        root = sb("root", [P, PACK], F32)
-        nc.gpsimd.tensor_tensor(root[:], root0[:], corr[:], ALU.mult)
+        nc.scalar.activation(corr[:], near_one[:], ACT.Copy, scale=-0.5, bias=1.5)
+        root = times("root", root0, corr)
 
         v_sc = sb("v_sc", [P, S], U8)
         nc.vector.tensor_copy(v_sc[:], tab_sc[:].bitcast(U8).indirect(offsets[:]))
@@ -232,16 +221,27 @@ def tile_list_campaign_interaction_logits_kernel(
         sq = {}
 
         def squares(q):
-            sq[q] = sb(f"sq{q}", [P, PACK, QUART], F32)
+            if q == 2:
+                sq[q] = staged(f"sq{q}", [P, PACK, QUART], F32, "g")
+            else:
+                sq[q] = sb(f"sq{q}", [P, PACK, QUART], F32)
             for t in range(PACK):
                 nc.scalar.activation(sq[q][:, t, :], banks_a[q, t], ACT.Square, scale=root[:, t : t + 1])
 
         squares(0)
-        for q in range(1, 4):
+        product_a(1)
+        squares(1)
+        wo_bf = staged("wo_bf", [P, N, PACK], BF16, "e")
+        nc.scalar.activation(
+            wo_bf[:].rearrange("p (c i) t -> p c t i", i=4),
+            wo_raw[:].rearrange("p t (c i) -> p c t i", i=4),
+            ACT.Copy,
+        )
+        for q in range(2, 4):
             product_a(q)
             squares(q)
 
-        h_bf = {q: sb(f"h_bf{q}", [P, QUART, PACK], BF16) for q in range(2)}
+        h_bf = {q: sb(f"h_bf{q}", [P, QUART, PACK], BF16) for q in range(3)}
         h_w = [sb(f"h_w{q}", [P, QUART], U32) for q in range(4)]
         h_sc = [sb(f"h_sc{q}", [P, QUART], U8) for q in range(4)]
         res = [sb(f"res{q}", [P, 2, QUART], F32) for q in range(4)]
@@ -249,24 +249,14 @@ def tile_list_campaign_interaction_logits_kernel(
         wo_sc = sb("wo_sc", [P, N], U8)
         out_v = out.rearrange("(u p) j -> p u j", p=P)
 
-        def subtract(q, j0=0):
+        def subtract(q):
             c, lo = q // 2, (q % 2) * QUART
             nc.vector.tensor_tensor(
-                h_bf[q][:, j0:, :].rearrange("p (c i) t -> p c t i", i=4),
-                sq[q][:, :, j0:].rearrange("p t (c i) -> p c t i", i=4),
-                hb[c][:, :, lo + j0 : lo + QUART].rearrange("p t (c i) -> p c t i", i=4),
+                h_bf[q][:].rearrange("p (c i) t -> p c t i", i=4),
+                sq[q][:].rearrange("p t (c i) -> p c t i", i=4),
+                hb[c][:, :, lo : lo + QUART].rearrange("p t (c i) -> p c t i", i=4),
                 ALU.subtract,
             )
-
-        def subtract_gpsimd(q, j1):
-            c, lo = q // 2, (q % 2) * QUART
-            for j in range(0, j1, P):
-                nc.gpsimd.tensor_tensor(
-                    h_bf[q][:, j : j + P, :],
-                    sq[q][:, :, j : j + P].rearrange("p t j -> p j t"),
-                    hb[c][:, :, lo + j : lo + j + P].rearrange("p t j -> p j t"),
-                    ALU.subtract,
-                )
 
         def quant_h(q):
             nc.vector.quantize_mx(
@@ -290,24 +280,17 @@ def tile_list_campaign_interaction_logits_kernel(
             nc.sync.dma_start(out_v[:, :, cols], res[q][:])
 
         nc.vector.tensor_copy(g_pick[:, 1, :], g_tab[1][:].indirect(offsets[:]))
-        subtract_gpsimd(0, QUART)
-        subtract_gpsimd(1, P)
-        wo_bf = staged("wo_bf", [P, N, PACK], BF16, "e")
-        nc.vector.tensor_copy(
-            wo_bf[:].rearrange("p (c i) t -> p c t i", i=4),
-            wo_raw[:].rearrange("p t (c i) -> p c t i", i=4),
-        )
+        subtract(0)
+        subtract(1)
         quant_h(0)
         nc.vector.quantize_mx(
             out=wo_w[:].bitcast(FP8X4), scales=wo_sc[:], in_=wo_bf[:].rearrange("p n t -> p (n t)")
         )
-        subtract(1, P)
-        h_bf[2] = staged("h_bf2", [P, QUART, PACK], BF16, "g")
         subtract(2)
         quant_h(1)
-        quant_h(2)
         h_bf[3] = staged("h_bf3", [P, QUART, PACK], BF16, "e")
         subtract(3)
+        quant_h(2)
         finish(0)
         quant_h(3)
         finish(1)

@@ -19,8 +19,12 @@ ACT = mybir.ActivationFunctionType
 P = 128
 PACK = 4
 PASSES = K // (P * PACK)
-HALF = 512
-QUART = 256
+BLOCK_ROWS = 8
+QUADS = 4
+LIST_ROWS = 16
+HALF = S // 2
+QUART = S // 4
+RUN = 2
 
 
 def tile_list_campaign_interaction_logits_kernel(
@@ -29,188 +33,186 @@ def tile_list_campaign_interaction_logits_kernel(
     nc = tc.nc
     with ExitStack() as ctx:
         keep = ctx.enter_context(tc.tile_pool(name="keep", bufs=1))
-        stage = ctx.enter_context(tc.tile_pool(name="stage", bufs=1))
+        shared = ctx.enter_context(tc.tile_pool(name="shared", bufs=1))
         psum = ctx.enter_context(tc.psum_pool(name="psum", bufs=1))
 
-        def sb(name, shape, dtype):
+        def kept(name, shape, dtype):
             return keep.tile(shape, dtype, name=name, align_bytes=64)
 
-        offsets = keep.tile([P, S // 16], U16, name="offsets")
+        def reused(name, shape, dtype, buffer):
+            return shared.tile(shape, dtype, name=name, tag=buffer, align_bytes=64)
+
+        offsets = keep.tile([P, S // LIST_ROWS], U16, name="offsets")
         nc.sync.dma_start(offsets[:], offs)
 
-        def staged(name, shape, dtype, tag):
-            return stage.tile(shape, dtype, name=name, tag=tag, align_bytes=64)
-
-        wb_sc_raw = staged("wb_sc_raw", [P, PASSES, H // 4], I32, "d")
-        wb_sc = sb("wb_sc", [P, PACK, PASSES, P // 4], I32)
-        nc.vector.memset(wb_sc[:], 0)
-        v_sc1 = sb("v_sc1", [P, S // 4], I32)
+        wb_sc_raw = reused("wb_sc_raw", [P, PASSES, H // 4], I32, "wb_scales")
+        nc.vector.memset(wb_sc_raw[:], 0)
+        v_sc1 = kept("v_sc1", [P, S // 4], I32)
         nc.vector.memset(v_sc1[:], 0)
 
-        hw_pad = sb("hw_pad", [P, PACK, 8], F32)
-        hw_hbm = hw.rearrange("(g t i o) -> t g i o", t=PACK, i=8, o=1)
+        hw_pad = kept("hw_pad", [P, PACK, 8], F32)
+        hw_hbm = hw.rearrange("(b t i o) -> t b i o", t=PACK, i=BLOCK_ROWS, o=1)
         with nc.allow_non_contiguous_dma(reason="one channel weight per partition and slot"):
             for t in range(PACK):
                 nc.gpsimd.dma_start(hw_pad[:, t, 0:1], hw_hbm[t])
         hw_t = hw_pad[:, :, 0]
-        tab_sc = staged("tab_sc", [P, T // 4], I32, "a")
+
+        tab_sc = reused("tab_sc", [P, T // 4], I32, "tab_scales")
         tab_rows = tab_scales.bitcast(I32).rearrange("a r c -> (a r) c")
         nc.sync.dma_start(tab_sc[0:32, :], tab_rows)
-        for q in range(1, 4):
+        for q in range(1, QUADS):
             nc.sync.dma_start(
                 tab_sc[32 * q : 32 * q + 32, :],
                 tab_rows[4 * q : 4 * q + 4, :].unsqueeze(0).broadcast_to([8, 4, T // 4]),
             )
-        tab_w = [staged(f"tab_w{a}", [P, T], I32, "bc"[a]) for a in range(PASSES)]
-        wb_raw = staged("wb_raw", [P, PASSES, H // 2], I32, "f")
+        tab_w = [reused(f"tab_w{a}", [P, T], I32, f"table{a}") for a in range(PASSES)]
+        wb_raw = reused("wb_raw", [P, PASSES, H // 2], I32, "weights")
         nc.sync.dma_start(wb_raw[:], wb_words.bitcast(I32).rearrange("a p c -> p a c"))
-        nc.sync.dma_start(tab_w[0][:], tab_words[0].rearrange("p t i -> p (t i)").bitcast(I32))
+        nc.sync.dma_start(tab_w[0][:], tab_words[0].rearrange("p c i -> p (c i)").bitcast(I32))
         wb_sc_hbm = wb_scales.bitcast(I32).rearrange("a r c -> r a c")
-        for q in range(4):
+        for q in range(QUADS):
             nc.sync.dma_start(wb_sc_raw[32 * q : 32 * q + 4, :, :], wb_sc_hbm[4 * q : 4 * q + 4])
-        nc.sync.dma_start(tab_w[1][:], tab_words[1].rearrange("p t i -> p (t i)").bitcast(I32))
+        nc.sync.dma_start(tab_w[1][:], tab_words[1].rearrange("p c i -> p (c i)").bitcast(I32))
 
-        rs = sb("rs", [P, PACK], F32)
-        nc.scalar.activation(rs[:], hw_t, ACT.Abs_reciprocal_sqrt)
+        inv_root = kept("inv_root", [P, PACK], F32)
+        nc.scalar.activation(inv_root[:], hw_t, ACT.Abs_reciprocal_sqrt)
 
         def times(name, x, y):
-            prod = sb(name, [P, PACK], F32)
+            prod = kept(name, [P, PACK], F32)
             for t in range(PACK):
                 nc.scalar.activation(prod[:, t : t + 1], x[:, t : t + 1], ACT.Copy, scale=y[:, t : t + 1])
             return prod
 
-        root0 = times("root0", hw_t, rs)
-        near_one = times("near_one", root0, rs)
-        corr = sb("corr", [P, PACK], F32)
-        nc.scalar.activation(corr[:], near_one[:], ACT.Copy, scale=-0.5, bias=1.5)
-        root = times("root", root0, corr)
+        rough_root = times("rough_root", hw_t, inv_root)
+        near_one = times("near_one", rough_root, inv_root)
+        correction = kept("correction", [P, PACK], F32)
+        nc.scalar.activation(correction[:], near_one[:], ACT.Copy, scale=-0.5, bias=1.5)
+        root = times("root", rough_root, correction)
 
-        v_sc = sb("v_sc", [P, S], U8)
-        nc.vector.tensor_copy(v_sc[:], tab_sc[:].bitcast(U8).indirect(offsets[:]))
-        for q in range(4):
-            nc.sync.dma_start(v_sc1[32 * q : 32 * q + 4, :], v_sc[16 + 4 * q : 20 + 4 * q, :].bitcast(I32))
+        v_sc0 = kept("v_sc0", [P, S], U8)
+        nc.vector.tensor_copy(v_sc0[:], tab_sc[:].bitcast(U8).indirect(offsets[:]))
+        for q in range(QUADS):
+            nc.sync.dma_start(v_sc1[32 * q : 32 * q + 4, :], v_sc0[16 + 4 * q : 20 + 4 * q, :].bitcast(I32))
+        v_sc = [v_sc0[:], v_sc1[:].bitcast(U8)]
 
         def load_g(u):
-            rows = staged(f"g_tab{u}", [P, T], F32, "bc"[u])
+            rows = reused(f"g_tab{u}", [P, T], F32, f"table{u}")
             nc.sync.dma_start(rows[:], gT[u * P : (u + 1) * P, :])
             return rows
 
-        v = {}
+        v_w = {}
 
-        def gather_words(a, c, dst):
-            v[a, c] = dst
-            nc.vector.tensor_copy(dst, tab_w[a][:].bitcast(U32).indirect(offsets[:, 32 * c : 32 * (c + 1)]))
+        def gather_words(a, half, dst):
+            v_w[a, half] = dst
+            entries = slice(half * HALF // LIST_ROWS, (half + 1) * HALF // LIST_ROWS)
+            nc.vector.tensor_copy(dst, tab_w[a][:].bitcast(U32).indirect(offsets[:, entries]))
 
-        wb_w = staged("wb_w", [P, PACK, PASSES, P // 2], I32, "a")
+        wb_w = reused("wb_w", [P, PACK, PASSES, P // 2], I32, "tab_scales")
         nc.vector.tensor_copy(
-            wb_w[:].rearrange("p t a (g w) -> p t (a g) w", w=4),
-            wb_raw[:].rearrange("p a (g t w) -> p t (a g) w", t=PACK, w=4),
+            wb_w[:].rearrange("p t a (b w) -> p t (a b) w", w=4),
+            wb_raw[:].rearrange("p a (b t w) -> p t (a b) w", t=PACK, w=4),
         )
-        wa_raw = staged("wa_raw", [P, PASSES, PACK, H], F32, "f")
+        wa_raw = reused("wa_raw", [P, PASSES, PACK, H], F32, "weights")
         for a in range(PASSES):
             nc.sync.dma_start(
                 wa_raw[:, a], wa[a * P * PACK : (a + 1) * P * PACK, :].rearrange("(p j) c -> p j c", j=PACK)
             )
-        gather_words(0, 0, sb("v00", [P, HALF], U32)[:])
-        for q in range(4):
-            rows = slice(32 * q, 32 * q + 4)
-            nc.vector.tensor_copy(
-                wb_sc[rows].rearrange("p t a (g w) -> p t (a g) w", w=2),
-                wb_sc_raw[rows].rearrange("p a (g t w) -> p t (a g) w", t=PACK, w=2),
-            )
-        v_mid = staged("v_mid", [P, 2, HALF], U32, "d")
+        gather_words(0, 0, kept("v_first", [P, HALF], U32)[:])
+        wb_sc = kept("wb_sc", [P, PACK, PASSES, P // 4], I32)
+        nc.vector.tensor_copy(
+            wb_sc[:].rearrange("p t a (b w) -> p t (a b) w", w=2),
+            wb_sc_raw[:].rearrange("p a (b t w) -> p t (a b) w", t=PACK, w=2),
+        )
+        v_mid = reused("v_mid", [P, 2, HALF], U32, "wb_scales")
         gather_words(1, 0, v_mid[:, 0, :])
         gather_words(0, 1, v_mid[:, 1, :])
         g_tab = [load_g(0)]
-        gather_words(1, 1, sb("v11", [P, HALF], U32)[:])
+        gather_words(1, 1, kept("v_last", [P, HALF], U32)[:])
         g_tab.append(load_g(1))
 
-        banks_b = {}
+        b_banks = {}
 
-        def product_b(c):
-            cols = slice(c * HALF, (c + 1) * HALF)
-            for t, a in [(t, a) for t in range(PACK) for a in range(PASSES)]:
-                if a == 0:
-                    banks_b[c, t] = psum.tile([P, HALF], F32, name=f"b{c}{t}", tag=f"bank{t}")
-                nc.tensor.matmul_mx(
-                    out=banks_b[c, t][:],
-                    lhsT=wb_w[:, t, a, :].bitcast(FP4X4),
-                    lhsT_scale=wb_sc[:, t, a, :].bitcast(U8),
-                    rhs=v[a, c].bitcast(FP8X4),
-                    rhs_scale=v_sc[:, cols] if a == 0 else v_sc1[:].bitcast(U8)[:, cols],
-                    start=(a == 0),
-                    stop=(a == PASSES - 1),
-                )
-
-        hb = [sb(f"hb{c}", [P, PACK, HALF], F32) for c in range(2)]
-
-        def weigh_b(c):
+        def product_b(half):
+            cols = slice(half * HALF, (half + 1) * HALF)
             for t in range(PACK):
-                nc.scalar.activation(hb[c][:, t, :], banks_b[c, t][:], ACT.Copy, scale=hw_t[:, t : t + 1])
+                b_banks[half, t] = psum.tile([P, HALF], F32, name=f"b{half}{t}", tag=f"bank{t}")
+                for a in range(PASSES):
+                    nc.tensor.matmul_mx(
+                        out=b_banks[half, t][:],
+                        lhsT=wb_w[:, t, a, :].bitcast(FP4X4),
+                        lhsT_scale=wb_sc[:, t, a, :].bitcast(U8),
+                        rhs=v_w[a, half].bitcast(FP8X4),
+                        rhs_scale=v_sc[a][:, cols],
+                        start=(a == 0),
+                        stop=(a == PASSES - 1),
+                    )
 
-        product_b(0)
-        weigh_b(0)
-        product_b(1)
-        weigh_b(1)
+        hw_b = [kept(f"hw_b{half}", [P, PACK, HALF], F32) for half in range(2)]
+
+        def weigh_b(half):
+            for t in range(PACK):
+                nc.scalar.activation(hw_b[half][:, t, :], b_banks[half, t][:], ACT.Copy, scale=hw_pad[:, t, 0:1])
+
+        for half in range(2):
+            product_b(half)
+            weigh_b(half)
 
         wa_w = {}
         wa_sc = {}
-        pieces = [(0, 0, 2), (0, 2, 4), (1, 0, 2), (1, 2, 4)]
-        wa_bf = {}
-        for a, lo, hi in pieces:
-            if (a, lo) == (0, 0):
-                wa_bf[a, lo] = staged(f"wa_bf{a}{lo}", [P, hi - lo, P, PACK], BF16, "g")
-            else:
-                wa_bf[a, lo] = sb(f"wa_bf{a}{lo}", [P, hi - lo, P, PACK], BF16)
+        wa_bf = {(0, 0): reused("wa_bf00", [P, 2, P, PACK], BF16, "late")}
+        for a, u in ((0, 1), (1, 0), (1, 1)):
+            wa_bf[a, u] = kept(f"wa_bf{a}{u}", [P, 2, P, PACK], BF16)
 
-        def wa_round(a, lo, hi, t0, t1):
-            nc.vector.tensor_copy(
-                wa_bf[a, lo][:, t0 - lo : t1 - lo].rearrange("p t (g i) j -> p t g i j", i=8),
-                wa_raw[:, a].rearrange("p j (g t i) -> p t g i j", t=PACK, i=8)[:, t0:t1],
-            )
+        def round_wa(a, u):
+            runs = BLOCK_ROWS // RUN
+            src = wa_raw[:, a].rearrange("p j (b t c i) -> p t b c j i", t=PACK, c=runs, i=RUN)
+            dst = wa_bf[a, u][:].rearrange("p t (b c i) j -> p t b c j i", c=runs, i=RUN)
+            for t in range(2):
+                nc.vector.tensor_copy(dst[:, t], src[:, 2 * u + t])
 
-        def wa_quant(a, lo, hi):
-            codes = sb(f"wa_w{a}{lo}", [P, hi - lo, P], U32)
-            scales = sb(f"wa_sc{a}{lo}", [P, hi - lo, P], U8)
+        def quantize_wa(a, u):
+            codes = kept(f"wa_w{a}{u}", [P, 2, P], U32)
+            scales = kept(f"wa_sc{a}{u}", [P, 2, P], U8)
             nc.vector.quantize_mx(
                 out=codes[:].rearrange("p t m -> p (t m)").bitcast(FP8X4),
                 scales=scales[:].rearrange("p t m -> p (t m)"),
-                in_=wa_bf[a, lo][:].rearrange("p t m j -> p (t m j)"),
+                in_=wa_bf[a, u][:].rearrange("p t m j -> p (t m j)"),
             )
-            for t in range(lo, hi):
-                wa_w[a, t] = codes[:, t - lo, :]
-                wa_sc[a, t] = scales[:, t - lo, :]
+            for t in range(2):
+                wa_w[a, 2 * u + t] = codes[:, t, :]
+                wa_sc[a, 2 * u + t] = scales[:, t, :]
 
-        wa_round(0, 0, 2, 0, 2)
-        wa_round(0, 2, 4, 2, 4)
-        wa_quant(0, 0, 2)
-        wo_raw = staged("wo_raw", [P, PACK, N], F32, "g")
-        wo_hbm = wo.rearrange("(g t i) n -> t g i n", t=PACK, i=8)
+        round_wa(0, 0)
+        round_wa(0, 1)
+        quantize_wa(0, 0)
+        wo_raw = reused("wo_raw", [P, PACK, N], F32, "late")
+        wo_hbm = wo.rearrange("(b t i) n -> t b i n", t=PACK, i=BLOCK_ROWS)
         for t in range(PACK):
             nc.sync.dma_start(wo_raw[:, t, :], wo_hbm[t])
-        wa_round(1, 0, 2, 0, 2)
-        wa_quant(0, 2, 4)
-        wa_quant(1, 0, 2)
-        wa_round(1, 2, 4, 2, 4)
-        g_pick = sb("g_pick", [P, 2, S], F32)
-        wa_quant(1, 2, 4)
+        round_wa(1, 0)
+        quantize_wa(0, 1)
+        quantize_wa(1, 0)
+        round_wa(1, 1)
+        g_pick = kept("g_pick", [P, 2, S], F32)
+        quantize_wa(1, 1)
 
-        banks_a = {}
+        a_groups = {}
 
-        def product_a(q):
-            c, lo = q // 2, (q % 2) * QUART
-            cols = slice(q * QUART, (q + 1) * QUART)
+        def product_a(quart):
+            half, lo = quart // 2, (quart % 2) * QUART
+            cols = slice(quart * QUART, (quart + 1) * QUART)
             for t in range(PACK):
                 if t % 2 == 0:
-                    bank = psum.tile([P, 2, QUART], F32, name=f"a{q}{t}", tag=f"bank{(4 + 2 * q + t // 2) % 8}")
-                banks_a[q, t] = bank[:, t % 2, :]
+                    bank_no = (4 + 2 * quart + t // 2) % 8
+                    bank = psum.tile([P, 2, QUART], F32, name=f"a{quart}{t}", tag=f"bank{bank_no}")
+                a_groups[quart, t] = bank[:, t % 2, :]
                 for a in range(PASSES):
                     nc.tensor.matmul_mx(
-                        out=banks_a[q, t],
+                        out=a_groups[quart, t],
                         lhsT=wa_w[a, t].bitcast(FP8X4),
                         lhsT_scale=wa_sc[a, t],
-                        rhs=v[a, c][:, lo : lo + QUART].bitcast(FP8X4),
-                        rhs_scale=v_sc[:, cols] if a == 0 else v_sc1[:].bitcast(U8)[:, cols],
+                        rhs=v_w[a, half][:, lo : lo + QUART].bitcast(FP8X4),
+                        rhs_scale=v_sc[a][:, cols],
                         start=(a == 0),
                         stop=(a == PASSES - 1),
                     )
@@ -218,81 +220,81 @@ def tile_list_campaign_interaction_logits_kernel(
         product_a(0)
         nc.vector.tensor_copy(g_pick[:, 0, :], g_tab[0][:].indirect(offsets[:]))
 
-        sq = {}
+        hw_a2 = {}
 
-        def squares(q):
-            if q == 2:
-                sq[q] = staged(f"sq{q}", [P, PACK, QUART], F32, "g")
-            else:
-                sq[q] = sb(f"sq{q}", [P, PACK, QUART], F32)
+        def square_a(quart, dst):
+            hw_a2[quart] = dst
             for t in range(PACK):
-                nc.scalar.activation(sq[q][:, t, :], banks_a[q, t], ACT.Square, scale=root[:, t : t + 1])
+                nc.scalar.activation(dst[:, t, :], a_groups[quart, t], ACT.Square, scale=root[:, t : t + 1])
 
-        squares(0)
+        def side_by_side(ap):
+            return ap.rearrange("p (c i) t -> p c t i", i=RUN)
+
+        def by_slot(ap):
+            return ap.rearrange("p t (c i) -> p c t i", i=RUN)
+
+        square_a(0, kept("hw_a2_0", [P, PACK, QUART], F32))
         product_a(1)
-        squares(1)
-        wo_bf = staged("wo_bf", [P, N, PACK], BF16, "e")
-        nc.scalar.activation(
-            wo_bf[:].rearrange("p (c i) t -> p c t i", i=4),
-            wo_raw[:].rearrange("p t (c i) -> p c t i", i=4),
-            ACT.Copy,
-        )
-        for q in range(2, 4):
-            product_a(q)
-            squares(q)
+        square_a(1, kept("hw_a2_1", [P, PACK, QUART], F32))
+        wo_bf = reused("wo_bf", [P, N, PACK], BF16, "rounded")
+        nc.scalar.activation(side_by_side(wo_bf[:]), by_slot(wo_raw[:]), ACT.Copy)
+        product_a(2)
+        square_a(2, reused("hw_a2_2", [P, PACK, QUART], F32, "late"))
+        product_a(3)
+        square_a(3, kept("hw_a2_3", [P, PACK, QUART], F32))
 
-        h_bf = {q: sb(f"h_bf{q}", [P, QUART, PACK], BF16) for q in range(3)}
-        h_w = [sb(f"h_w{q}", [P, QUART], U32) for q in range(4)]
-        h_sc = [sb(f"h_sc{q}", [P, QUART], U8) for q in range(4)]
-        res = [sb(f"res{q}", [P, 2, QUART], F32) for q in range(4)]
-        wo_w = sb("wo_w", [P, N], U32)
-        wo_sc = sb("wo_sc", [P, N], U8)
-        out_v = out.rearrange("(u p) j -> p u j", p=P)
+        h_bf = [kept(f"h_bf{quart}", [P, QUART, PACK], BF16) for quart in range(3)]
+        h_w = [kept(f"h_w{quart}", [P, QUART], U32) for quart in range(4)]
+        h_sc = [kept(f"h_sc{quart}", [P, QUART], U8) for quart in range(4)]
+        result = [kept(f"result{quart}", [P, 2, QUART], F32) for quart in range(4)]
+        wo_w = kept("wo_w", [P, N], U32)
+        wo_sc = kept("wo_sc", [P, N], U8)
+        out_view = out.rearrange("(u p) j -> p u j", p=P)
 
-        def subtract(q):
-            c, lo = q // 2, (q % 2) * QUART
+        def subtract(quart):
+            half, lo = quart // 2, (quart % 2) * QUART
             nc.vector.tensor_tensor(
-                h_bf[q][:].rearrange("p (c i) t -> p c t i", i=4),
-                sq[q][:].rearrange("p t (c i) -> p c t i", i=4),
-                hb[c][:, :, lo : lo + QUART].rearrange("p t (c i) -> p c t i", i=4),
+                side_by_side(h_bf[quart][:]),
+                by_slot(hw_a2[quart][:]),
+                by_slot(hw_b[half][:, :, lo : lo + QUART]),
                 ALU.subtract,
             )
 
-        def quant_h(q):
+        def quantize_h(quart):
             nc.vector.quantize_mx(
-                out=h_w[q][:].bitcast(FP8X4), scales=h_sc[q][:], in_=h_bf[q][:].rearrange("p j t -> p (j t)")
+                out=h_w[quart][:].bitcast(FP8X4),
+                scales=h_sc[quart][:],
+                in_=h_bf[quart][:].rearrange("p j t -> p (j t)"),
             )
 
-        def finish(q):
-            cols = slice(q * QUART, (q + 1) * QUART)
-            y = psum.tile([P, 2, QUART], F32, name=f"y{q}", tag=f"bank{4 + q}")
+        def finish(quart):
+            cols = slice(quart * QUART, (quart + 1) * QUART)
+            y = psum.tile([P, 2, QUART], F32, name=f"y{quart}", tag=f"bank{4 + quart}")
             for u in range(2):
                 nc.tensor.matmul_mx(
                     out=y[:, u, :],
                     lhsT=wo_w[:, u * P : (u + 1) * P].bitcast(FP8X4),
                     lhsT_scale=wo_sc[:, u * P : (u + 1) * P],
-                    rhs=h_w[q][:].bitcast(FP8X4),
-                    rhs_scale=h_sc[q][:],
+                    rhs=h_w[quart][:].bitcast(FP8X4),
+                    rhs_scale=h_sc[quart][:],
                     start=True,
                     stop=True,
                 )
-            nc.vector.scalar_tensor_tensor(res[q][:], y[:], 0.5, g_pick[:, :, cols], ALU.mult, ALU.add)
-            nc.sync.dma_start(out_v[:, :, cols], res[q][:])
+            nc.vector.scalar_tensor_tensor(result[quart][:], y[:], 0.5, g_pick[:, :, cols], ALU.mult, ALU.add)
+            nc.sync.dma_start(out_view[:, :, cols], result[quart][:])
 
         nc.vector.tensor_copy(g_pick[:, 1, :], g_tab[1][:].indirect(offsets[:]))
         subtract(0)
         subtract(1)
-        quant_h(0)
+        quantize_h(0)
         nc.vector.quantize_mx(
             out=wo_w[:].bitcast(FP8X4), scales=wo_sc[:], in_=wo_bf[:].rearrange("p n t -> p (n t)")
         )
         subtract(2)
-        quant_h(1)
-        h_bf[3] = staged("h_bf3", [P, QUART, PACK], BF16, "e")
+        quantize_h(1)
+        h_bf.append(reused("h_bf3", [P, QUART, PACK], BF16, "rounded"))
         subtract(3)
-        quant_h(2)
-        finish(0)
-        quant_h(3)
-        finish(1)
-        finish(2)
-        finish(3)
+        quantize_h(2)
+        quantize_h(3)
+        for quart in range(4):
+            finish(quart)

@@ -1,6 +1,7 @@
 from contextlib import ExitStack
 
 import concourse.mybir as mybir
+from concourse.masks import make_identity
 
 K, H, N, T, S = 1024, 512, 256, 2048, 1024
 FLOPS = 2 * K * H * S * 2 + 2 * H * N * S
@@ -50,12 +51,10 @@ def tile_list_campaign_interaction_logits_kernel(
         v_sc1 = kept("v_sc1", [P, S // 4], I32)
         nc.vector.memset(v_sc1[:], 0)
 
-        hw_pad = kept("hw_pad", [P, PACK, 8], F32)
-        hw_hbm = hw.rearrange("(b t i o) -> t b i o", t=PACK, i=BLOCK_ROWS, o=1)
-        with nc.allow_non_contiguous_dma(reason="one channel weight per partition and slot"):
-            for t in range(PACK):
-                nc.gpsimd.dma_start(hw_pad[:, t, 0:1], hw_hbm[t])
-        hw_t = hw_pad[:, :, 0]
+        hw_rows = kept("hw_rows", [P, P], F32)
+        nc.gpsimd.memset(hw_rows[:], 0.0)
+        identity = kept("identity", [P, P], F32)
+        make_identity(nc, identity[:])
 
         tab_sc = reused("tab_sc", [P, T // 4], I32, "tab_scales")
         tab_rows = tab_scales.bitcast(I32).rearrange("a r c -> (a r) c")
@@ -74,8 +73,17 @@ def tile_list_campaign_interaction_logits_kernel(
             nc.sync.dma_start(wb_sc_raw[32 * q : 32 * q + 4, :, :], wb_sc_hbm[4 * q : 4 * q + 4])
         nc.sync.dma_start(tab_w[1][:], tab_words[1].rearrange("p c i -> p (c i)").bitcast(I32))
 
+        nc.scalar.dma_start(
+            hw_rows[0:PACK, :].rearrange("t (b i) -> t b i", i=BLOCK_ROWS),
+            hw.rearrange("(b t i) -> t b i", t=PACK, i=BLOCK_ROWS),
+        )
+        hw_turned = psum.tile([P, P], F32, name="hw_turned", tag="bank7")
+        nc.tensor.transpose(hw_turned[:], hw_rows[:], identity[:])
+        hw_t = kept("hw_t", [P, PACK], F32)
+        nc.scalar.copy(hw_t[:], hw_turned[:, 0:PACK])
+
         inv_root = kept("inv_root", [P, PACK], F32)
-        nc.scalar.activation(inv_root[:], hw_t, ACT.Abs_reciprocal_sqrt)
+        nc.scalar.activation(inv_root[:], hw_t[:], ACT.Abs_reciprocal_sqrt)
 
         def times(name, x, y):
             prod = kept(name, [P, PACK], F32)
@@ -112,22 +120,27 @@ def tile_list_campaign_interaction_logits_kernel(
             wb_w[:].rearrange("p t a (b w) -> p t (a b) w", w=4),
             wb_raw[:].rearrange("p a (b t w) -> p t (a b) w", t=PACK, w=4),
         )
-        wa_raw = reused("wa_raw", [P, PASSES, PACK, H], F32, "weights")
+        weights = reused("weights", [P, PASSES * PACK * H + PACK * N], F32, "weights")
+        wa_raw = weights[:, : PASSES * PACK * H].rearrange("p (a j c) -> p a j c", a=PASSES, j=PACK)
         for a in range(PASSES):
             nc.sync.dma_start(
                 wa_raw[:, a], wa[a * P * PACK : (a + 1) * P * PACK, :].rearrange("(p j) c -> p j c", j=PACK)
             )
+        wo_raw = weights[:, PASSES * PACK * H :].rearrange("p (t n) -> p t n", t=PACK)
+        wo_hbm = wo.rearrange("(b t i) n -> t b i n", t=PACK, i=BLOCK_ROWS)
+        for t in range(PACK):
+            nc.sync.dma_start(wo_raw[:, t, :], wo_hbm[t])
         gather_words(0, 0, kept("v_first", [P, HALF], U32)[:])
         wb_sc = kept("wb_sc", [P, PACK, PASSES, P // 4], I32)
         nc.vector.tensor_copy(
             wb_sc[:].rearrange("p t a (b w) -> p t (a b) w", w=2),
             wb_sc_raw[:].rearrange("p a (b t w) -> p t (a b) w", t=PACK, w=2),
         )
-        v_mid = reused("v_mid", [P, 2, HALF], U32, "wb_scales")
-        gather_words(1, 0, v_mid[:, 0, :])
-        gather_words(0, 1, v_mid[:, 1, :])
+        v_rest = reused("v_rest", [P, 3, HALF], U32, "wb_scales")
+        gather_words(0, 1, v_rest[:, 0, :])
         g_tab = [load_g(0)]
-        gather_words(1, 1, kept("v_last", [P, HALF], U32)[:])
+        gather_words(1, 0, v_rest[:, 1, :])
+        gather_words(1, 1, v_rest[:, 2, :])
         g_tab.append(load_g(1))
 
         b_banks = {}
@@ -151,7 +164,7 @@ def tile_list_campaign_interaction_logits_kernel(
 
         def weigh_b(half):
             for t in range(PACK):
-                nc.scalar.activation(hw_b[half][:, t, :], b_banks[half, t][:], ACT.Copy, scale=hw_pad[:, t, 0:1])
+                nc.scalar.activation(hw_b[half][:, t, :], b_banks[half, t][:], ACT.Copy, scale=hw_t[:, t : t + 1])
 
         for half in range(2):
             product_b(half)
@@ -159,8 +172,8 @@ def tile_list_campaign_interaction_logits_kernel(
 
         wa_w = {}
         wa_sc = {}
-        wa_bf = {(0, 0): reused("wa_bf00", [P, 2, P, PACK], BF16, "late")}
-        for a, u in ((0, 1), (1, 0), (1, 1)):
+        wa_bf = {}
+        for a, u in ((0, 0), (0, 1), (1, 0), (1, 1)):
             wa_bf[a, u] = kept(f"wa_bf{a}{u}", [P, 2, P, PACK], BF16)
 
         def round_wa(a, u):
@@ -185,15 +198,10 @@ def tile_list_campaign_interaction_logits_kernel(
         round_wa(0, 0)
         round_wa(0, 1)
         quantize_wa(0, 0)
-        wo_raw = reused("wo_raw", [P, PACK, N], F32, "late")
-        wo_hbm = wo.rearrange("(b t i) n -> t b i n", t=PACK, i=BLOCK_ROWS)
-        for t in range(PACK):
-            nc.sync.dma_start(wo_raw[:, t, :], wo_hbm[t])
         round_wa(1, 0)
         quantize_wa(0, 1)
         quantize_wa(1, 0)
         round_wa(1, 1)
-        g_pick = kept("g_pick", [P, 2, S], F32)
         quantize_wa(1, 1)
 
         a_groups = {}
@@ -202,10 +210,7 @@ def tile_list_campaign_interaction_logits_kernel(
             half, lo = quart // 2, (quart % 2) * QUART
             cols = slice(quart * QUART, (quart + 1) * QUART)
             for t in range(PACK):
-                if t % 2 == 0:
-                    bank_no = (4 + 2 * quart + t // 2) % 8
-                    bank = psum.tile([P, 2, QUART], F32, name=f"a{quart}{t}", tag=f"bank{bank_no}")
-                a_groups[quart, t] = bank[:, t % 2, :]
+                a_groups[quart, t] = psum.tile([P, QUART], F32, name=f"a{quart}{t}", tag=f"bank{4 + t}")[:]
                 for a in range(PASSES):
                     nc.tensor.matmul_mx(
                         out=a_groups[quart, t],
@@ -217,15 +222,12 @@ def tile_list_campaign_interaction_logits_kernel(
                         stop=(a == PASSES - 1),
                     )
 
-        product_a(0)
-        nc.vector.tensor_copy(g_pick[:, 0, :], g_tab[0][:].indirect(offsets[:]))
-
         hw_a2 = {}
 
-        def square_a(quart, dst):
-            hw_a2[quart] = dst
+        def square_a(quart):
+            hw_a2[quart] = reused(f"hw_a2_{quart}", [P, PACK, QUART], F32, f"square{quart}")
             for t in range(PACK):
-                nc.scalar.activation(dst[:, t, :], a_groups[quart, t], ACT.Square, scale=root[:, t : t + 1])
+                nc.scalar.activation(hw_a2[quart][:, t, :], a_groups[quart, t], ACT.Square, scale=root[:, t : t + 1])
 
         def side_by_side(ap):
             return ap.rearrange("p (c i) t -> p c t i", i=RUN)
@@ -233,26 +235,21 @@ def tile_list_campaign_interaction_logits_kernel(
         def by_slot(ap):
             return ap.rearrange("p t (c i) -> p c t i", i=RUN)
 
-        square_a(0, kept("hw_a2_0", [P, PACK, QUART], F32))
-        product_a(1)
-        square_a(1, kept("hw_a2_1", [P, PACK, QUART], F32))
-        wo_bf = reused("wo_bf", [P, N, PACK], BF16, "rounded")
-        nc.scalar.activation(side_by_side(wo_bf[:]), by_slot(wo_raw[:]), ACT.Copy)
-        product_a(2)
-        square_a(2, reused("hw_a2_2", [P, PACK, QUART], F32, "late"))
-        product_a(3)
-        square_a(3, kept("hw_a2_3", [P, PACK, QUART], F32))
+        wo_bf = kept("wo_bf", [P, N, PACK], BF16)
+        nc.vector.tensor_copy(side_by_side(wo_bf[:]), by_slot(wo_raw))
+        for quart in range(4):
+            product_a(quart)
+            square_a(quart)
 
-        h_bf = [kept(f"h_bf{quart}", [P, QUART, PACK], BF16) for quart in range(3)]
-        h_w = [kept(f"h_w{quart}", [P, QUART], U32) for quart in range(4)]
+        h_bf = {}
+        h_w = {}
         h_sc = [kept(f"h_sc{quart}", [P, QUART], U8) for quart in range(4)]
-        result = [kept(f"result{quart}", [P, 2, QUART], F32) for quart in range(4)]
-        wo_w = kept("wo_w", [P, N], U32)
-        wo_sc = kept("wo_sc", [P, N], U8)
+        half_y = {}
         out_view = out.rearrange("(u p) j -> p u j", p=P)
 
         def subtract(quart):
             half, lo = quart // 2, (quart % 2) * QUART
+            h_bf[quart] = reused(f"h_bf{quart}", [P, QUART, PACK], BF16, f"rounded{quart}")
             nc.vector.tensor_tensor(
                 side_by_side(h_bf[quart][:]),
                 by_slot(hw_a2[quart][:]),
@@ -260,16 +257,16 @@ def tile_list_campaign_interaction_logits_kernel(
                 ALU.subtract,
             )
 
-        def quantize_h(quart):
+        def quantize_h(quart, buffer):
+            h_w[quart] = reused(f"h_w{quart}", [P, QUART], U32, buffer)
             nc.vector.quantize_mx(
                 out=h_w[quart][:].bitcast(FP8X4),
                 scales=h_sc[quart][:],
                 in_=h_bf[quart][:].rearrange("p j t -> p (j t)"),
             )
 
-        def finish(quart):
-            cols = slice(quart * QUART, (quart + 1) * QUART)
-            y = psum.tile([P, 2, QUART], F32, name=f"y{quart}", tag=f"bank{4 + quart}")
+        def product_y(quart):
+            y = psum.tile([P, 2, QUART], F32, name=f"y{quart}", tag=f"bank{quart}")
             for u in range(2):
                 nc.tensor.matmul_mx(
                     out=y[:, u, :],
@@ -280,21 +277,37 @@ def tile_list_campaign_interaction_logits_kernel(
                     start=True,
                     stop=True,
                 )
-            nc.vector.scalar_tensor_tensor(result[quart][:], y[:], 0.5, g_pick[:, :, cols], ALU.mult, ALU.add)
-            nc.sync.dma_start(out_view[:, :, cols], result[quart][:])
+            half_y[quart] = reused(f"half_y{quart}", [P, 2, QUART], F32, f"half{quart}")
+            nc.scalar.activation(half_y[quart][:], y[:], ACT.Copy, scale=0.5)
 
-        nc.vector.tensor_copy(g_pick[:, 1, :], g_tab[1][:].indirect(offsets[:]))
+        def finish(quart, buffer):
+            cols = slice(quart * QUART, (quart + 1) * QUART)
+            entries = slice(quart * QUART // LIST_ROWS, (quart + 1) * QUART // LIST_ROWS)
+            result = reused(f"result{quart}", [P, 2, QUART], F32, buffer)
+            for u in range(2):
+                nc.vector.tensor_tensor(
+                    result[:, u, :], g_tab[u][:].indirect(offsets[:, entries]), half_y[quart][:, u, :], ALU.add
+                )
+            nc.sync.dma_start(out_view[:, :, cols], result[:])
+
         subtract(0)
-        subtract(1)
-        quantize_h(0)
+        wo_w = reused("wo_w", [P, N], U32, "square0")
+        wo_sc = kept("wo_sc", [P, N], U8)
         nc.vector.quantize_mx(
             out=wo_w[:].bitcast(FP8X4), scales=wo_sc[:], in_=wo_bf[:].rearrange("p n t -> p (n t)")
         )
+        subtract(1)
+        quantize_h(0, "square1")
+        product_y(0)
         subtract(2)
-        quantize_h(1)
-        h_bf.append(reused("h_bf3", [P, QUART, PACK], BF16, "rounded"))
+        quantize_h(1, "square2")
+        product_y(1)
         subtract(3)
-        quantize_h(2)
-        quantize_h(3)
-        for quart in range(4):
-            finish(quart)
+        quantize_h(2, "square3")
+        product_y(2)
+        finish(0, "result0")
+        quantize_h(3, "half0")
+        product_y(3)
+        finish(1, "rounded3")
+        finish(2, "result2")
+        finish(3, "result3")

@@ -96,6 +96,9 @@ def tile_list_campaign_interaction_logits_kernel(
         correction = kept("correction", [P, PACK], F32)
         nc.scalar.activation(correction[:], near_one[:], ACT.Copy, scale=-0.5, bias=1.5)
         root = times("root", rough_root, correction)
+        roots = [reused(f"root{quart}", [P, PACK], F32, f"root{quart}") for quart in range(4)]
+        for quart in range(4):
+            nc.scalar.copy(roots[quart][:], root[:])
 
         v_sc0 = kept("v_sc0", [P, S], U8)
         nc.vector.tensor_copy(v_sc0[:], tab_sc[:].bitcast(U8).indirect(offsets[:]))
@@ -115,7 +118,7 @@ def tile_list_campaign_interaction_logits_kernel(
             entries = slice(half * HALF // LIST_ROWS, (half + 1) * HALF // LIST_ROWS)
             nc.vector.tensor_copy(dst, tab_w[a][:].bitcast(U32).indirect(offsets[:, entries]))
 
-        wb_w = reused("wb_w", [P, PACK, PASSES, P // 2], I32, "tab_scales")
+        wb_w = kept("wb_w", [P, PACK, PASSES, P // 2], I32)
         nc.vector.tensor_copy(
             wb_w[:].rearrange("p t a (b w) -> p t (a b) w", w=4),
             wb_raw[:].rearrange("p a (b t w) -> p t (a b) w", t=PACK, w=4),
@@ -225,9 +228,9 @@ def tile_list_campaign_interaction_logits_kernel(
         hw_a2 = {}
 
         def square_a(quart):
-            hw_a2[quart] = reused(f"hw_a2_{quart}", [P, PACK, QUART], F32, f"square{quart}")
+            hw_a2[quart] = kept(f"hw_a2_{quart}", [P, PACK, QUART], F32)
             for t in range(PACK):
-                nc.scalar.activation(hw_a2[quart][:, t, :], a_groups[quart, t], ACT.Square, scale=root[:, t : t + 1])
+                nc.scalar.activation(hw_a2[quart][:, t, :], a_groups[quart, t], ACT.Square, scale=roots[quart][:, t : t + 1])
 
         def side_by_side(ap):
             return ap.rearrange("p (c i) t -> p c t i", i=RUN)
@@ -288,26 +291,29 @@ def tile_list_campaign_interaction_logits_kernel(
                 nc.vector.tensor_tensor(
                     result[:, u, :], g_tab[u][:].indirect(offsets[:, entries]), half_y[quart][:, u, :], ALU.add
                 )
-            nc.sync.dma_start(out_view[:, :, cols], result[:])
+                if quart == 3:
+                    nc.sync.dma_start(out_view[:, u, cols], result[:, u, :])
+            if quart < 3:
+                nc.sync.dma_start(out_view[:, :, cols], result[:])
 
         subtract(0)
-        wo_w = reused("wo_w", [P, N], U32, "square0")
+        wo_w = reused("wo_w", [P, N], U32, "root0")
         wo_sc = kept("wo_sc", [P, N], U8)
         nc.vector.quantize_mx(
             out=wo_w[:].bitcast(FP8X4), scales=wo_sc[:], in_=wo_bf[:].rearrange("p n t -> p (n t)")
         )
         subtract(1)
-        quantize_h(0, "square1")
+        quantize_h(0, "root1")
         product_y(0)
         subtract(2)
-        quantize_h(1, "square2")
+        quantize_h(1, "root2")
         product_y(1)
         subtract(3)
-        quantize_h(2, "square3")
+        quantize_h(2, "root3")
         product_y(2)
         finish(0, "result0")
-        quantize_h(3, "half0")
+        quantize_h(3, "codes3")
         product_y(3)
-        finish(1, "rounded3")
+        finish(1, "root3")
         finish(2, "result2")
         finish(3, "result3")

@@ -186,26 +186,27 @@ def tile_list_campaign_interaction_logits_kernel(
             for t in range(2):
                 nc.vector.tensor_copy(dst[:, t], src[:, 2 * u + t])
 
-        def quantize_wa(a, u):
-            codes = kept(f"wa_w{a}{u}", [P, 2, P], U32)
-            scales = kept(f"wa_sc{a}{u}", [P, 2, P], U8)
+        def quantize_wa(a, u, first=0, count=2):
+            codes = kept(f"wa_w{a}{u}{first}", [P, count, P], U32)
+            scales = kept(f"wa_sc{a}{u}{first}", [P, count, P], U8)
             nc.vector.quantize_mx(
                 out=codes[:].rearrange("p t m -> p (t m)").bitcast(FP8X4),
                 scales=scales[:].rearrange("p t m -> p (t m)"),
-                in_=wa_bf[a, u][:].rearrange("p t m j -> p (t m j)"),
+                in_=wa_bf[a, u][:, first : first + count].rearrange("p t m j -> p (t m j)"),
             )
-            for t in range(2):
-                wa_w[a, 2 * u + t] = codes[:, t, :]
-                wa_sc[a, 2 * u + t] = scales[:, t, :]
+            for t in range(count):
+                wa_w[a, 2 * u + first + t] = codes[:, t, :]
+                wa_sc[a, 2 * u + first + t] = scales[:, t, :]
 
         round_wa(0, 0)
         round_wa(0, 1)
         quantize_wa(0, 0)
-        round_wa(1, 0)
         quantize_wa(0, 1)
-        quantize_wa(1, 0)
+        round_wa(1, 0)
         round_wa(1, 1)
-        quantize_wa(1, 1)
+        quantize_wa(1, 0)
+        quantize_wa(1, 1, 0, 1)
+        quantize_wa(1, 1, 1, 1)
 
         a_groups = {}
 
@@ -213,16 +214,17 @@ def tile_list_campaign_interaction_logits_kernel(
             half, lo = quart // 2, (quart % 2) * QUART
             cols = slice(quart * QUART, (quart + 1) * QUART)
             for t in range(PACK):
-                a_groups[quart, t] = psum.tile([P, QUART], F32, name=f"a{quart}{t}", tag=f"bank{4 + t}")[:]
-                for a in range(PASSES):
+                a_groups[quart, t] = psum.tile([P, QUART], F32, name=f"a{quart}{t}", tag=f"bank{4 * (1 - quart % 2) + t}")[:]
+                order = (0, 1) if quart == 0 else (1, 0)
+                for a in order:
                     nc.tensor.matmul_mx(
                         out=a_groups[quart, t],
                         lhsT=wa_w[a, t].bitcast(FP8X4),
                         lhsT_scale=wa_sc[a, t],
                         rhs=v_w[a, half][:, lo : lo + QUART].bitcast(FP8X4),
                         rhs_scale=v_sc[a][:, cols],
-                        start=(a == 0),
-                        stop=(a == PASSES - 1),
+                        start=(a == order[0]),
+                        stop=(a == order[-1]),
                     )
 
         hw_a2 = {}
@@ -240,6 +242,11 @@ def tile_list_campaign_interaction_logits_kernel(
 
         wo_bf = kept("wo_bf", [P, N, PACK], BF16)
         nc.vector.tensor_copy(side_by_side(wo_bf[:]), by_slot(wo_raw))
+        wo_w = kept("wo_w", [P, N], U32)
+        wo_sc = kept("wo_sc", [P, N], U8)
+        nc.vector.quantize_mx(
+            out=wo_w[:].bitcast(FP8X4), scales=wo_sc[:], in_=wo_bf[:].rearrange("p n t -> p (n t)")
+        )
         for quart in range(4):
             product_a(quart)
             square_a(quart)
@@ -269,7 +276,7 @@ def tile_list_campaign_interaction_logits_kernel(
             )
 
         def product_y(quart):
-            y = psum.tile([P, 2, QUART], F32, name=f"y{quart}", tag=f"bank{quart}")
+            y = psum.tile([P, 2, QUART], F32, name=f"y{quart}", tag=f"bank{4 + quart}")
             for u in range(2):
                 nc.tensor.matmul_mx(
                     out=y[:, u, :],
@@ -297,11 +304,6 @@ def tile_list_campaign_interaction_logits_kernel(
                 nc.sync.dma_start(out_view[:, :, cols], result[:])
 
         subtract(0)
-        wo_w = reused("wo_w", [P, N], U32, "root0")
-        wo_sc = kept("wo_sc", [P, N], U8)
-        nc.vector.quantize_mx(
-            out=wo_w[:].bitcast(FP8X4), scales=wo_sc[:], in_=wo_bf[:].rearrange("p n t -> p (n t)")
-        )
         subtract(1)
         quantize_h(0, "root1")
         product_y(0)

@@ -60,7 +60,8 @@ def tile_list_campaign_interaction_logits_kernel(
         tab_rows = tab_scales.bitcast(I32).rearrange("a r c -> (a r) c")
         nc.sync.dma_start(tab_sc[0:32, :], tab_rows)
         for q in range(1, QUADS):
-            nc.sync.dma_start(
+            queue = nc.sync if q == 1 else nc.scalar
+            queue.dma_start(
                 tab_sc[32 * q : 32 * q + 32, :],
                 tab_rows[4 * q : 4 * q + 4, :].unsqueeze(0).broadcast_to([8, 4, T // 4]),
             )
@@ -313,9 +314,9 @@ def tile_list_campaign_interaction_logits_kernel(
         subtract(3)
         quantize_h(2, "root3")
         product_y(2)
-        finish(0, "result0")
         quantize_h(3, "codes3")
         product_y(3)
-        finish(1, "root3")
+        finish(0, "result0")
+        finish(1, "result1")
         finish(2, "result2")
         finish(3, "result3")

@@ -26,6 +26,7 @@ LIST_ROWS = 16
 HALF = S // 2
 QUART = S // 4
 RUN = 2
+LAST = 64
 
 
 def tile_list_campaign_interaction_logits_kernel(
@@ -97,9 +98,14 @@ def tile_list_campaign_interaction_logits_kernel(
         correction = kept("correction", [P, PACK], F32)
         nc.scalar.activation(correction[:], near_one[:], ACT.Copy, scale=-0.5, bias=1.5)
         root = times("root", rough_root, correction)
-        roots = [reused(f"root{quart}", [P, PACK], F32, f"root{quart}") for quart in range(4)]
-        for quart in range(4):
+        roots = {}
+
+        def copy_root(quart, buffer):
+            roots[quart] = reused(f"root{quart}", [P, PACK], F32, buffer)
             nc.scalar.copy(roots[quart][:], root[:])
+
+        for quart in range(4):
+            copy_root(quart, f"root{quart}")
 
         v_sc0 = kept("v_sc0", [P, S], U8)
         nc.vector.tensor_copy(v_sc0[:], tab_sc[:].bitcast(U8).indirect(offsets[:]))
@@ -114,10 +120,13 @@ def tile_list_campaign_interaction_logits_kernel(
 
         v_w = {}
 
-        def gather_words(a, half, dst):
+        def gather_words(a, half, dst, pieces=1):
             v_w[a, half] = dst
-            entries = slice(half * HALF // LIST_ROWS, (half + 1) * HALF // LIST_ROWS)
-            nc.vector.tensor_copy(dst, tab_w[a][:].bitcast(U32).indirect(offsets[:, entries]))
+            width = HALF // pieces
+            for lo in range(0, HALF, width):
+                first = half * HALF + lo
+                entries = slice(first // LIST_ROWS, (first + width) // LIST_ROWS)
+                nc.vector.tensor_copy(dst[:, lo : lo + width], tab_w[a][:].bitcast(U32).indirect(offsets[:, entries]))
 
         wb_w = kept("wb_w", [P, PACK, PASSES, P // 2], I32)
         nc.vector.tensor_copy(
@@ -143,48 +152,45 @@ def tile_list_campaign_interaction_logits_kernel(
         v_rest = reused("v_rest", [P, 3, HALF], U32, "wb_scales")
         gather_words(0, 1, v_rest[:, 0, :])
         g_tab = [load_g(0)]
-        gather_words(1, 0, v_rest[:, 1, :])
+        gather_words(1, 0, v_rest[:, 1, :], pieces=2)
         gather_words(1, 1, v_rest[:, 2, :])
         g_tab.append(load_g(1))
 
-        b_banks = {}
-
-        def product_b(half):
-            cols = slice(half * HALF, (half + 1) * HALF)
-            for t in range(PACK):
-                b_banks[half, t] = psum.tile([P, HALF], F32, name=f"b{half}{t}", tag=f"bank{t}")
-                for a in range(PASSES):
-                    nc.tensor.matmul_mx(
-                        out=b_banks[half, t][:],
-                        lhsT=wb_w[:, t, a, :].bitcast(FP4X4),
-                        lhsT_scale=wb_sc[:, t, a, :].bitcast(U8),
-                        rhs=v_w[a, half].bitcast(FP8X4),
-                        rhs_scale=v_sc[a][:, cols],
-                        start=(a == 0),
-                        stop=(a == PASSES - 1),
-                    )
-
         hw_b = [kept(f"hw_b{half}", [P, PACK, HALF], F32) for half in range(2)]
 
-        def weigh_b(half):
+        def weighted_b(first, width, step, bank):
+            half, lo = first // HALF, first % HALF
+            groups = [psum.tile([P, width], F32, name=f"b{first}_{t}", tag=f"bank{bank + t}") for t in range(PACK)]
             for t in range(PACK):
-                nc.scalar.activation(hw_b[half][:, t, :], b_banks[half, t][:], ACT.Copy, scale=hw_t[:, t : t + 1])
+                for a in range(PASSES):
+                    for c in range(0, width, step):
+                        nc.tensor.matmul_mx(
+                            out=groups[t][:, c : c + step],
+                            lhsT=wb_w[:, t, a, :].bitcast(FP4X4),
+                            lhsT_scale=wb_sc[:, t, a, :].bitcast(U8),
+                            rhs=v_w[a, half][:, lo + c : lo + c + step].bitcast(FP8X4),
+                            rhs_scale=v_sc[a][:, first + c : first + c + step],
+                            start=(a == 0 and c == 0),
+                            stop=(a == PASSES - 1 and c == width - step),
+                        )
+            for t in range(PACK):
+                nc.scalar.activation(hw_b[half][:, t, lo : lo + width], groups[t][:], ACT.Copy, scale=hw_t[:, t : t + 1])
 
-        for half in range(2):
-            product_b(half)
-            weigh_b(half)
+        weighted_b(0, QUART, P, 0)
+        weighted_b(QUART, QUART, P, 4)
+        weighted_b(HALF, HALF, HALF, 0)
 
         wa_w = {}
         wa_sc = {}
         wa_bf = {}
         for a, u in ((0, 0), (0, 1), (1, 0), (1, 1)):
-            wa_bf[a, u] = kept(f"wa_bf{a}{u}", [P, 2, P, PACK], BF16)
+            wa_bf[a, u] = reused(f"wa_bf{a}{u}", [P, 2, P, PACK], BF16, f"wa_bf{a}{u}")
 
-        def round_wa(a, u):
+        def round_wa(a, u, slots=range(2)):
             runs = BLOCK_ROWS // RUN
             src = wa_raw[:, a].rearrange("p j (b t c i) -> p t b c j i", t=PACK, c=runs, i=RUN)
             dst = wa_bf[a, u][:].rearrange("p t (b c i) j -> p t b c j i", c=runs, i=RUN)
-            for t in range(2):
+            for t in slots:
                 nc.vector.tensor_copy(dst[:, t], src[:, 2 * u + t])
 
         def quantize_wa(a, u, first=0, count=2):
@@ -204,18 +210,25 @@ def tile_list_campaign_interaction_logits_kernel(
         quantize_wa(0, 0)
         quantize_wa(0, 1)
         round_wa(1, 0)
-        round_wa(1, 1)
-        quantize_wa(1, 0)
+        quantize_wa(1, 0, 0, 1)
+        round_wa(1, 1, [0])
+        quantize_wa(1, 0, 1, 1)
+        round_wa(1, 1, [1])
         quantize_wa(1, 1, 0, 1)
         quantize_wa(1, 1, 1, 1)
 
         a_groups = {}
 
-        def product_a(quart):
+        def product_a(quart, slots):
             half, lo = quart // 2, (quart % 2) * QUART
             cols = slice(quart * QUART, (quart + 1) * QUART)
-            for t in range(PACK):
-                a_groups[quart, t] = psum.tile([P, QUART], F32, name=f"a{quart}{t}", tag=f"bank{4 * (1 - quart % 2) + t}")[:]
+            if quart == 1:
+                for t in range(2):
+                    both = psum.tile([P, 2, QUART], F32, name=f"a{quart}{t}", tag=f"bank{t}")
+                    a_groups[quart, t], a_groups[quart, PACK - 1 - t] = both[:, 0, :], both[:, 1, :]
+            for t in slots:
+                if quart != 1:
+                    a_groups[quart, t] = psum.tile([P, QUART], F32, name=f"a{quart}{t}", tag=f"bank{4 * (1 - quart % 2) + t}")[:]
                 order = (0, 1) if quart == 0 else (1, 0)
                 for a in order:
                     nc.tensor.matmul_mx(
@@ -228,11 +241,10 @@ def tile_list_campaign_interaction_logits_kernel(
                         stop=(a == order[-1]),
                     )
 
-        hw_a2 = {}
+        hw_a2 = [kept(f"hw_a2_{quart}", [P, PACK, QUART], F32) for quart in range(4)]
 
-        def square_a(quart):
-            hw_a2[quart] = kept(f"hw_a2_{quart}", [P, PACK, QUART], F32)
-            for t in range(PACK):
+        def square_a(quart, slots):
+            for t in slots:
                 nc.scalar.activation(hw_a2[quart][:, t, :], a_groups[quart, t], ACT.Square, scale=roots[quart][:, t : t + 1])
 
         def side_by_side(ap):
@@ -243,14 +255,9 @@ def tile_list_campaign_interaction_logits_kernel(
 
         wo_bf = kept("wo_bf", [P, N, PACK], BF16)
         nc.vector.tensor_copy(side_by_side(wo_bf[:]), by_slot(wo_raw))
-        wo_w = kept("wo_w", [P, N], U32)
-        wo_sc = kept("wo_sc", [P, N], U8)
-        nc.vector.quantize_mx(
-            out=wo_w[:].bitcast(FP8X4), scales=wo_sc[:], in_=wo_bf[:].rearrange("p n t -> p (n t)")
-        )
         for quart in range(4):
-            product_a(quart)
-            square_a(quart)
+            product_a(quart, (1, 2, 0, 3) if quart == 1 else range(PACK))
+            square_a(quart, (1, 2, 0, 3) if quart == 1 else range(PACK))
 
         h_bf = {}
         h_w = {}
@@ -293,18 +300,27 @@ def tile_list_campaign_interaction_logits_kernel(
 
         def finish(quart, buffer):
             cols = slice(quart * QUART, (quart + 1) * QUART)
-            entries = slice(quart * QUART // LIST_ROWS, (quart + 1) * QUART // LIST_ROWS)
             result = reused(f"result{quart}", [P, 2, QUART], F32, buffer)
-            for u in range(2):
+            pieces = [(0, 0, QUART), (1, 0, QUART)]
+            if quart == 3:
+                pieces = [(0, 0, QUART), (1, 0, QUART - LAST), (1, QUART - LAST, QUART)]
+            for u, lo, hi in pieces:
+                first, last = quart * QUART + lo, quart * QUART + hi
+                entries = offsets[:, first // LIST_ROWS : last // LIST_ROWS]
                 nc.vector.tensor_tensor(
-                    result[:, u, :], g_tab[u][:].indirect(offsets[:, entries]), half_y[quart][:, u, :], ALU.add
+                    result[:, u, lo:hi], g_tab[u][:].indirect(entries), half_y[quart][:, u, lo:hi], ALU.add
                 )
                 if quart == 3:
-                    nc.sync.dma_start(out_view[:, u, cols], result[:, u, :])
+                    nc.sync.dma_start(out_view[:, u, first:last], result[:, u, lo:hi])
             if quart < 3:
                 nc.sync.dma_start(out_view[:, :, cols], result[:])
 
         subtract(0)
+        wo_w = reused("wo_w", [P, N], U32, "root0")
+        wo_sc = kept("wo_sc", [P, N], U8)
+        nc.vector.quantize_mx(
+            out=wo_w[:].bitcast(FP8X4), scales=wo_sc[:], in_=wo_bf[:].rearrange("p n t -> p (n t)")
+        )
         subtract(1)
         quantize_h(0, "root1")
         product_y(0)

@@ -83,6 +83,8 @@ def tile_list_campaign_interaction_logits_kernel(
         nc.tensor.transpose(hw_turned[:], hw_rows[:], identity[:])
         hw_t = kept("hw_t", [P, PACK], F32)
         nc.scalar.copy(hw_t[:], hw_turned[:, 0:PACK])
+        minus_hw = kept("minus_hw", [P, PACK], F32)
+        nc.scalar.activation(minus_hw[:], hw_turned[:, 0:PACK], ACT.Copy, scale=-1.0)
 
         inv_root = kept("inv_root", [P, PACK], F32)
         nc.scalar.activation(inv_root[:], hw_t[:], ACT.Abs_reciprocal_sqrt)
@@ -174,7 +176,7 @@ def tile_list_campaign_interaction_logits_kernel(
                             stop=(a == PASSES - 1 and c == width - step),
                         )
             for t in range(PACK):
-                nc.scalar.activation(hw_b[half][:, t, lo : lo + width], groups[t][:], ACT.Copy, scale=hw_t[:, t : t + 1])
+                nc.scalar.activation(hw_b[half][:, t, lo : lo + width], groups[t][:], ACT.Copy, scale=minus_hw[:, t : t + 1])
 
         weighted_b(0, QUART, P, 0)
         weighted_b(QUART, QUART, P, 4)
@@ -265,14 +267,14 @@ def tile_list_campaign_interaction_logits_kernel(
         half_y = {}
         out_view = out.rearrange("(u p) j -> p u j", p=P)
 
-        def subtract(quart):
+        def subtract(quart, width=QUART):
             half, lo = quart // 2, (quart % 2) * QUART
             h_bf[quart] = reused(f"h_bf{quart}", [P, QUART, PACK], BF16, f"rounded{quart}")
             nc.vector.tensor_tensor(
-                side_by_side(h_bf[quart][:]),
-                by_slot(hw_a2[quart][:]),
-                by_slot(hw_b[half][:, :, lo : lo + QUART]),
-                ALU.subtract,
+                side_by_side(h_bf[quart][:, :width]),
+                by_slot(hw_a2[quart][:, :, :width]),
+                by_slot(hw_b[half][:, :, lo : lo + width]),
+                ALU.add,
             )
 
         def quantize_h(quart, buffer):
@@ -283,8 +285,28 @@ def tile_list_campaign_interaction_logits_kernel(
                 in_=h_bf[quart][:].rearrange("p j t -> p (j t)"),
             )
 
+        def subtract_by_transposes(quart, first):
+            half, lo = quart // 2, (quart % 2) * QUART + first
+            sums = psum.tile([P, PACK, P], F32, name="h_turned", tag="bank7")
+            for t in range(PACK):
+                minus_b = hw_b[half][:, t, lo : lo + P]
+                nc.tensor.matmul(sums[:, t, :], minus_b, identity[:], start=(t == 0), stop=False, is_transpose=True)
+            for t in range(PACK):
+                square = hw_a2[quart][:, t, first : first + P]
+                nc.tensor.matmul(sums[:, t, :], square, identity[:], start=False, stop=(t == PACK - 1), is_transpose=True)
+            pairs = reused("h_pairs", [P, 2, P, 2], BF16, "pairs")
+            nc.scalar.copy(pairs[:], sums[:].rearrange("j (u e) p -> j u p e", e=2))
+            words = psum.tile([P, 2, P], F32, name="h_words", tag="bank1")
+            for u in range(2):
+                nc.tensor.transpose(words[:, u, :], pairs[:, u].rearrange("j p e -> j (p e)").bitcast(F32), identity[:])
+            return words
+
+        def copy_words(quart, first, words):
+            side = h_bf[quart][:, first : first + P].rearrange("p j t -> p (j t)").bitcast(F32)
+            nc.scalar.copy(side.rearrange("p (j u) -> p j u", u=2), words[:].rearrange("p u j -> p j u"))
+
         def product_y(quart):
-            y = psum.tile([P, 2, QUART], F32, name=f"y{quart}", tag=f"bank{4 + quart}")
+            y = psum.tile([P, 2, QUART], F32, name=f"y{quart}", tag=f"bank{(4, 5, 6, 0)[quart]}")
             for u in range(2):
                 nc.tensor.matmul_mx(
                     out=y[:, u, :],
@@ -295,8 +317,12 @@ def tile_list_campaign_interaction_logits_kernel(
                     start=True,
                     stop=True,
                 )
-            half_y[quart] = reused(f"half_y{quart}", [P, 2, QUART], F32, f"half{quart}")
-            nc.scalar.activation(half_y[quart][:], y[:], ACT.Copy, scale=0.5)
+            return y
+
+        def halve(quart, y, dst, groups=slice(0, 2)):
+            nc.scalar.activation(dst, y[:, groups, :], ACT.Copy, scale=0.5)
+            for u in range(groups.start, groups.stop):
+                half_y[quart, u] = dst[:, u - groups.start, :]
 
         def finish(quart, buffer):
             cols = slice(quart * QUART, (quart + 1) * QUART)
@@ -308,7 +334,7 @@ def tile_list_campaign_interaction_logits_kernel(
                 first, last = quart * QUART + lo, quart * QUART + hi
                 entries = offsets[:, first // LIST_ROWS : last // LIST_ROWS]
                 nc.vector.tensor_tensor(
-                    result[:, u, lo:hi], g_tab[u][:].indirect(entries), half_y[quart][:, u, lo:hi], ALU.add
+                    result[:, u, lo:hi], g_tab[u][:].indirect(entries), half_y[quart, u][:, lo:hi], ALU.add
                 )
                 if quart == 3:
                     nc.sync.dma_start(out_view[:, u, first:last], result[:, u, lo:hi])
@@ -323,15 +349,22 @@ def tile_list_campaign_interaction_logits_kernel(
         )
         subtract(1)
         quantize_h(0, "root1")
-        product_y(0)
+        halve(0, product_y(0), kept("half_y0", [P, 2, QUART], F32)[:])
         subtract(2)
         quantize_h(1, "root2")
-        product_y(1)
-        subtract(3)
+        subtract(3, P)
         quantize_h(2, "root3")
-        product_y(2)
+        words = subtract_by_transposes(3, P)
+        y1 = product_y(1)
+        halve(1, y1, kept("half_y10", [P, 1, QUART], F32)[:], slice(0, 1))
+        copy_words(3, P, words)
         quantize_h(3, "codes3")
-        product_y(3)
+        late = reused("half_y_late", [P, 3, QUART], F32, "pairs")
+        halve(1, y1, late[:, 0:1, :], slice(1, 2))
+        halve(2, product_y(2), late[:, 1:3, :])
+        y3 = product_y(3)
+        for u in range(2):
+            halve(3, y3, kept(f"half_y3{u}", [P, 1, QUART], F32)[:], slice(u, u + 1))
         finish(0, "result0")
         finish(1, "result1")
         finish(2, "result2")

@@ -185,39 +185,36 @@ def tile_list_campaign_interaction_logits_kernel(
         wa_w = {}
         wa_sc = {}
         wa_bf = {}
-        for a, u in ((0, 0), (0, 1), (1, 0), (1, 1)):
-            wa_bf[a, u] = reused(f"wa_bf{a}{u}", [P, 2, P, PACK], BF16, f"wa_bf{a}{u}")
 
-        def round_wa(a, u, slots=range(2)):
+        def round_wa(a, first, count):
+            wa_bf[a, first] = kept(f"wa_bf{a}{first}", [P, count, P, PACK], BF16)
             runs = BLOCK_ROWS // RUN
             src = wa_raw[:, a].rearrange("p j (b t c i) -> p t b c j i", t=PACK, c=runs, i=RUN)
-            dst = wa_bf[a, u][:].rearrange("p t (b c i) j -> p t b c j i", c=runs, i=RUN)
-            for t in slots:
-                nc.vector.tensor_copy(dst[:, t], src[:, 2 * u + t])
+            dst = wa_bf[a, first][:].rearrange("p t (b c i) j -> p t b c j i", c=runs, i=RUN)
+            for t in range(count):
+                nc.vector.tensor_copy(dst[:, t], src[:, first + t])
 
-        def quantize_wa(a, u, first=0, count=2):
-            codes = kept(f"wa_w{a}{u}{first}", [P, count, P], U32)
-            scales = kept(f"wa_sc{a}{u}{first}", [P, count, P], U8)
+        def quantize_wa(a, first, count):
+            codes = kept(f"wa_w{a}{first}", [P, count, P], U32)
+            scales = kept(f"wa_sc{a}{first}", [P, count, P], U8)
             nc.vector.quantize_mx(
                 out=codes[:].rearrange("p t m -> p (t m)").bitcast(FP8X4),
                 scales=scales[:].rearrange("p t m -> p (t m)"),
-                in_=wa_bf[a, u][:, first : first + count].rearrange("p t m j -> p (t m j)"),
+                in_=wa_bf[a, first][:].rearrange("p t m j -> p (t m j)"),
             )
             for t in range(count):
-                wa_w[a, 2 * u + first + t] = codes[:, t, :]
-                wa_sc[a, 2 * u + first + t] = scales[:, t, :]
+                wa_w[a, first + t] = codes[:, t, :]
+                wa_sc[a, first + t] = scales[:, t, :]
 
-        round_wa(0, 0)
-        round_wa(0, 1)
-        quantize_wa(0, 0)
-        quantize_wa(0, 1)
-        round_wa(1, 0)
-        quantize_wa(1, 0, 0, 1)
-        round_wa(1, 1, [0])
-        quantize_wa(1, 0, 1, 1)
-        round_wa(1, 1, [1])
-        quantize_wa(1, 1, 0, 1)
-        quantize_wa(1, 1, 1, 1)
+        for first in (0, 2):
+            round_wa(0, first, 2)
+        for first in (0, 2):
+            quantize_wa(0, first, 2)
+        round_wa(1, 0, 1)
+        for t in range(1, PACK):
+            round_wa(1, t, 1)
+            quantize_wa(1, t - 1, 1)
+        quantize_wa(1, PACK - 1, 1)
 
         a_groups = {}
 
@@ -255,8 +252,15 @@ def tile_list_campaign_interaction_logits_kernel(
         def by_slot(ap):
             return ap.rearrange("p t (c i) -> p c t i", i=RUN)
 
-        wo_bf = kept("wo_bf", [P, N, PACK], BF16)
-        nc.vector.tensor_copy(side_by_side(wo_bf[:]), by_slot(wo_raw))
+        wo_bf = [kept(f"wo_bf{u}", [P, P, PACK], BF16) for u in range(2)]
+        wo_w = [kept(f"wo_w{u}", [P, P], U32) for u in range(2)]
+        wo_sc = [kept(f"wo_sc{u}", [P, P], U8) for u in range(2)]
+        for u in range(2):
+            nc.vector.tensor_copy(side_by_side(wo_bf[u][:]), by_slot(wo_raw[:, :, u * P : (u + 1) * P]))
+        for u in range(2):
+            nc.vector.quantize_mx(
+                out=wo_w[u][:].bitcast(FP8X4), scales=wo_sc[u][:], in_=wo_bf[u][:].rearrange("p n t -> p (n t)")
+            )
         for quart in range(4):
             product_a(quart, (1, 2, 0, 3) if quart == 1 else range(PACK))
             square_a(quart, (1, 2, 0, 3) if quart == 1 else range(PACK))
@@ -310,8 +314,8 @@ def tile_list_campaign_interaction_logits_kernel(
             for u in range(2):
                 nc.tensor.matmul_mx(
                     out=y[:, u, :],
-                    lhsT=wo_w[:, u * P : (u + 1) * P].bitcast(FP8X4),
-                    lhsT_scale=wo_sc[:, u * P : (u + 1) * P],
+                    lhsT=wo_w[u][:].bitcast(FP8X4),
+                    lhsT_scale=wo_sc[u][:],
                     rhs=h_w[quart][:].bitcast(FP8X4),
                     rhs_scale=h_sc[quart][:],
                     start=True,
@@ -342,11 +346,6 @@ def tile_list_campaign_interaction_logits_kernel(
                 nc.sync.dma_start(out_view[:, :, cols], result[:])
 
         subtract(0)
-        wo_w = reused("wo_w", [P, N], U32, "root0")
-        wo_sc = kept("wo_sc", [P, N], U8)
-        nc.vector.quantize_mx(
-            out=wo_w[:].bitcast(FP8X4), scales=wo_sc[:], in_=wo_bf[:].rearrange("p n t -> p (n t)")
-        )
         subtract(1)
         quantize_h(0, "root1")
         halve(0, product_y(0), kept("half_y0", [P, 2, QUART], F32)[:])

@@ -120,15 +120,16 @@ def tile_list_campaign_interaction_logits_kernel(
             nc.sync.dma_start(rows[:], gT[u * P : (u + 1) * P, :])
             return rows
 
-        v_w = {}
+        def gather_words(a, first, width):
+            entries = slice(first // LIST_ROWS, (first + width) // LIST_ROWS)
+            nc.vector.tensor_copy(words_of(a, first, width), tab_w[a][:].bitcast(U32).indirect(offsets[:, entries]))
 
-        def gather_words(a, half, dst, pieces=1):
-            v_w[a, half] = dst
-            width = HALF // pieces
-            for lo in range(0, HALF, width):
-                first = half * HALF + lo
-                entries = slice(first // LIST_ROWS, (first + width) // LIST_ROWS)
-                nc.vector.tensor_copy(dst[:, lo : lo + width], tab_w[a][:].bitcast(U32).indirect(offsets[:, entries]))
+        def words_of(a, first, width):
+            if a * S + first < QUART:
+                return v_parts[0][:, first : first + width]
+            return v_parts[1][:, a * S + first - QUART : a * S + first - QUART + width]
+
+        v_parts = [kept("v_first", [P, QUART], U32)]
 
         wb_w = kept("wb_w", [P, PACK, PASSES, P // 2], I32)
         nc.vector.tensor_copy(
@@ -145,17 +146,18 @@ def tile_list_campaign_interaction_logits_kernel(
         wo_hbm = wo.rearrange("(b t i) n -> t b i n", t=PACK, i=BLOCK_ROWS)
         for t in range(PACK):
             nc.sync.dma_start(wo_raw[:, t, :], wo_hbm[t])
-        gather_words(0, 0, kept("v_first", [P, HALF], U32)[:])
+        gather_words(0, 0, QUART)
         wb_sc = kept("wb_sc", [P, PACK, PASSES, P // 4], I32)
         nc.vector.tensor_copy(
             wb_sc[:].rearrange("p t a (b w) -> p t (a b) w", w=2),
             wb_sc_raw[:].rearrange("p a (b t w) -> p t (a b) w", t=PACK, w=2),
         )
-        v_rest = reused("v_rest", [P, 3, HALF], U32, "wb_scales")
-        gather_words(0, 1, v_rest[:, 0, :])
+        v_parts.append(reused("v_rest", [P, 2 * S - QUART], U32, "wb_scales"))
+        gather_words(0, QUART, QUART)
+        gather_words(0, HALF, HALF)
         g_tab = [load_g(0)]
-        gather_words(1, 0, v_rest[:, 1, :], pieces=2)
-        gather_words(1, 1, v_rest[:, 2, :])
+        for first, width in ((0, QUART), (QUART, QUART), (HALF, HALF)):
+            gather_words(1, first, width)
         g_tab.append(load_g(1))
 
         hw_b = [kept(f"hw_b{half}", [P, PACK, HALF], F32) for half in range(2)]
@@ -170,7 +172,7 @@ def tile_list_campaign_interaction_logits_kernel(
                             out=groups[t][:, c : c + step],
                             lhsT=wb_w[:, t, a, :].bitcast(FP4X4),
                             lhsT_scale=wb_sc[:, t, a, :].bitcast(U8),
-                            rhs=v_w[a, half][:, lo + c : lo + c + step].bitcast(FP8X4),
+                            rhs=words_of(a, first + c, step).bitcast(FP8X4),
                             rhs_scale=v_sc[a][:, first + c : first + c + step],
                             start=(a == 0 and c == 0),
                             stop=(a == PASSES - 1 and c == width - step),
@@ -178,8 +180,8 @@ def tile_list_campaign_interaction_logits_kernel(
             for t in range(PACK):
                 nc.scalar.activation(hw_b[half][:, t, lo : lo + width], groups[t][:], ACT.Copy, scale=minus_hw[:, t : t + 1])
 
-        weighted_b(0, QUART, P, 0)
-        weighted_b(QUART, QUART, P, 4)
+        weighted_b(0, QUART, QUART, 0)
+        weighted_b(QUART, QUART, QUART, 4)
         weighted_b(HALF, HALF, HALF, 0)
 
         wa_w = {}
@@ -219,7 +221,6 @@ def tile_list_campaign_interaction_logits_kernel(
         a_groups = {}
 
         def product_a(quart, slots):
-            half, lo = quart // 2, (quart % 2) * QUART
             cols = slice(quart * QUART, (quart + 1) * QUART)
             if quart == 1:
                 for t in range(2):
@@ -234,7 +235,7 @@ def tile_list_campaign_interaction_logits_kernel(
                         out=a_groups[quart, t],
                         lhsT=wa_w[a, t].bitcast(FP8X4),
                         lhsT_scale=wa_sc[a, t],
-                        rhs=v_w[a, half][:, lo : lo + QUART].bitcast(FP8X4),
+                        rhs=words_of(a, quart * QUART, QUART).bitcast(FP8X4),
                         rhs_scale=v_sc[a][:, cols],
                         start=(a == order[0]),
                         stop=(a == order[-1]),

@@ -82,32 +82,27 @@ def tile_list_campaign_interaction_logits_kernel(
         hw_turned = psum.tile([P, P], F32, name="hw_turned", tag="bank7")
         nc.tensor.transpose(hw_turned[:], hw_rows[:], identity[:])
         hw_t = kept("hw_t", [P, PACK], F32)
-        nc.scalar.copy(hw_t[:], hw_turned[:, 0:PACK])
         minus_hw = kept("minus_hw", [P, PACK], F32)
-        nc.scalar.activation(minus_hw[:], hw_turned[:, 0:PACK], ACT.Copy, scale=-1.0)
 
         inv_root = kept("inv_root", [P, PACK], F32)
-        nc.scalar.activation(inv_root[:], hw_t[:], ACT.Abs_reciprocal_sqrt)
+        nc.scalar.activation(inv_root[:], hw_turned[:, 0:PACK], ACT.Abs_reciprocal_sqrt)
+        nc.scalar.copy(hw_t[:], hw_turned[:, 0:PACK])
+        nc.scalar.activation(minus_hw[:], hw_turned[:, 0:PACK], ACT.Copy, scale=-1.0)
 
-        def times(name, x, y):
-            prod = kept(name, [P, PACK], F32)
+        def times(prod, x, y, bias=0.0):
             for t in range(PACK):
-                nc.scalar.activation(prod[:, t : t + 1], x[:, t : t + 1], ACT.Copy, scale=y[:, t : t + 1])
-            return prod
+                nc.scalar.activation(prod[:, t : t + 1], x[:, t : t + 1], ACT.Copy, scale=y[:, t : t + 1], bias=bias)
 
-        rough_root = times("rough_root", hw_t, inv_root)
-        near_one = times("near_one", rough_root, inv_root)
+        minus_half_inv = kept("minus_half_inv", [P, PACK], F32)
+        nc.scalar.activation(minus_half_inv[:], inv_root[:], ACT.Copy, scale=-0.5)
+        rough_root = kept("rough_root", [P, PACK], F32)
+        times(rough_root, hw_t, inv_root)
         correction = kept("correction", [P, PACK], F32)
-        nc.scalar.activation(correction[:], near_one[:], ACT.Copy, scale=-0.5, bias=1.5)
-        root = times("root", rough_root, correction)
-        roots = {}
-
-        def copy_root(quart, buffer):
-            roots[quart] = reused(f"root{quart}", [P, PACK], F32, buffer)
-            nc.scalar.copy(roots[quart][:], root[:])
-
-        for quart in range(4):
-            copy_root(quart, f"root{quart}")
+        times(correction, rough_root, minus_half_inv, bias=1.5)
+        roots = [reused(f"root{quart}", [P, PACK], F32, f"root{quart}") for quart in range(4)]
+        times(roots[0], rough_root, correction)
+        for quart in range(1, 4):
+            nc.scalar.copy(roots[quart][:], roots[0][:])
 
         v_sc0 = kept("v_sc0", [P, S], U8)
         nc.vector.tensor_copy(v_sc0[:], tab_sc[:].bitcast(U8).indirect(offsets[:]))

@@ -47,7 +47,7 @@ def tile_list_campaign_interaction_logits_kernel(
         offsets = keep.tile([P, S // LIST_ROWS], U16, name="offsets")
         nc.sync.dma_start(offsets[:], offs)
 
-        wb_sc_raw = reused("wb_sc_raw", [P, PASSES, H // 4], I32, "wb_scales")
+        wb_sc_raw = kept("wb_sc_raw", [P, PASSES, H // 4], I32)
         nc.vector.memset(wb_sc_raw[:], 0)
         v_sc1 = kept("v_sc1", [P, S // 4], I32)
         nc.vector.memset(v_sc1[:], 0)
@@ -57,7 +57,7 @@ def tile_list_campaign_interaction_logits_kernel(
         identity = kept("identity", [P, P], F32)
         make_identity(nc, identity[:])
 
-        tab_sc = reused("tab_sc", [P, T // 4], I32, "tab_scales")
+        tab_sc = reused("tab_sc", [P, T // 4], I32, "weights")
         tab_rows = tab_scales.bitcast(I32).rearrange("a r c -> (a r) c")
         nc.sync.dma_start(tab_sc[0:32, :], tab_rows)
         for q in range(1, QUADS):
@@ -67,7 +67,7 @@ def tile_list_campaign_interaction_logits_kernel(
                 tab_rows[4 * q : 4 * q + 4, :].unsqueeze(0).broadcast_to([8, 4, T // 4]),
             )
         tab_w = [reused(f"tab_w{a}", [P, T], I32, f"table{a}") for a in range(PASSES)]
-        wb_raw = reused("wb_raw", [P, PASSES, H // 2], I32, "weights")
+        wb_raw = kept("wb_raw", [P, PASSES, H // 2], I32)
         nc.sync.dma_start(wb_raw[:], wb_words.bitcast(I32).rearrange("a p c -> p a c"))
         nc.sync.dma_start(tab_w[0][:], tab_words[0].rearrange("p c i -> p (c i)").bitcast(I32))
         wb_sc_hbm = wb_scales.bitcast(I32).rearrange("a r c -> r a c")
@@ -127,7 +127,7 @@ def tile_list_campaign_interaction_logits_kernel(
         v_parts = [kept("v_first", [P, QUART], U32)]
 
         wb_w = kept("wb_w", [P, PACK, PASSES, P // 2], I32)
-        nc.vector.tensor_copy(
+        nc.gpsimd.tensor_copy(
             wb_w[:].rearrange("p t a (b w) -> p t (a b) w", w=4),
             wb_raw[:].rearrange("p a (b t w) -> p t (a b) w", t=PACK, w=4),
         )
@@ -143,11 +143,11 @@ def tile_list_campaign_interaction_logits_kernel(
             nc.sync.dma_start(wo_raw[:, t, :], wo_hbm[t])
         gather_words(0, 0, QUART)
         wb_sc = kept("wb_sc", [P, PACK, PASSES, P // 4], I32)
-        nc.vector.tensor_copy(
+        nc.gpsimd.tensor_copy(
             wb_sc[:].rearrange("p t a (b w) -> p t (a b) w", w=2),
             wb_sc_raw[:].rearrange("p a (b t w) -> p t (a b) w", t=PACK, w=2),
         )
-        v_parts.append(reused("v_rest", [P, 2 * S - QUART], U32, "wb_scales"))
+        v_parts.append(kept("v_rest", [P, 2 * S - QUART], U32))
         gather_words(0, QUART, QUART)
         gather_words(0, HALF, HALF)
         g_tab = [load_g(0)]

@@ -1,7 +1,6 @@
 from contextlib import ExitStack
 
 import concourse.mybir as mybir
-from concourse.masks import make_identity
 
 K, H, N, T, S = 1024, 512, 256, 2048, 1024
 FLOPS = 2 * K * H * S * 2 + 2 * H * N * S
@@ -36,6 +35,7 @@ def tile_list_campaign_interaction_logits_kernel(
     with ExitStack() as ctx:
         keep = ctx.enter_context(tc.tile_pool(name="keep", bufs=1))
         shared = ctx.enter_context(tc.tile_pool(name="shared", bufs=1))
+        placed = ctx.enter_context(tc.tile_pool(name="placed", bufs=1))
         psum = ctx.enter_context(tc.psum_pool(name="psum", bufs=1))
 
         def kept(name, shape, dtype):
@@ -44,36 +44,66 @@ def tile_list_campaign_interaction_logits_kernel(
         def reused(name, shape, dtype, buffer):
             return shared.tile(shape, dtype, name=name, tag=buffer, align_bytes=64)
 
+        def laid(name, shape, dtype, offset):
+            return placed.tile(shape, dtype, name=name, align_bytes=64, offset=offset)
+
         offsets = keep.tile([P, S // LIST_ROWS], U16, name="offsets")
         nc.sync.dma_start(offsets[:], offs)
 
-        wb_sc_raw = kept("wb_sc_raw", [P, PASSES, H // 4], I32)
-        nc.vector.memset(wb_sc_raw[:], 0)
-        v_sc1 = kept("v_sc1", [P, S // 4], I32)
-        nc.vector.memset(v_sc1[:], 0)
+        tab_sc = kept("tab_sc", [P, T // 4], I32)
+        nc.gpsimd.memset(tab_sc[:], 0)
 
-        hw_rows = kept("hw_rows", [P, P], F32)
-        nc.gpsimd.memset(hw_rows[:], 0.0)
-        identity = kept("identity", [P, P], F32)
-        make_identity(nc, identity[:])
+        wb_raw = kept("wb_raw", [P, PASSES, H // 2], I32)
+        nc.sync.dma_start(wb_raw[:], wb_words.bitcast(I32).rearrange("a p c -> p a c"))
 
-        tab_sc = reused("tab_sc", [P, T // 4], I32, "weights")
         tab_rows = tab_scales.bitcast(I32).rearrange("a r c -> (a r) c")
         nc.sync.dma_start(tab_sc[0:32, :], tab_rows)
         for q in range(1, QUADS):
-            queue = nc.sync if q == 1 else nc.scalar
-            queue.dma_start(
-                tab_sc[32 * q : 32 * q + 32, :],
-                tab_rows[4 * q : 4 * q + 4, :].unsqueeze(0).broadcast_to([8, 4, T // 4]),
+            nc.sync.dma_start(tab_sc[32 * q : 32 * q + 4, :], tab_rows[4 * q : 4 * q + 4, :])
+
+        identity = kept("identity", [P, P], F32)
+
+        def cut_identity(ones, first):
+            width = ones.shape[1]
+            nc.gpsimd.affine_select(
+                out=identity[:, first : first + width],
+                in_=ones,
+                pattern=[[-1, width]],
+                compare_op=ALU.is_equal,
+                fill=0.0,
+                base=-first,
+                channel_multiplier=1,
             )
-        tab_w = [reused(f"tab_w{a}", [P, T], I32, f"table{a}") for a in range(PASSES)]
-        wb_raw = kept("wb_raw", [P, PASSES, H // 2], I32)
-        nc.sync.dma_start(wb_raw[:], wb_words.bitcast(I32).rearrange("a p c -> p a c"))
+
+        ones_left = laid("ones_left", [P, 4896], F32, 8128)
+        nc.vector.memset(ones_left[:, : P // 2], 1.0)
+        cut_identity(ones_left[:, : P // 2], 0)
+        wb_sc_raw = laid("wb_sc_raw", [P, PASSES, H // 4], I32, 27648)
+        nc.gpsimd.memset(wb_sc_raw[:], 0)
+        ones_right = laid("ones_right", [P, 2592], F32, 9152)
+        nc.gpsimd.memset(ones_right[:, : P // 2], 1.0)
+        cut_identity(ones_right[:, : P // 2], P // 2)
+        v_sc1 = laid("v_sc1", [P, S // 4], I32, 8192)
+        nc.gpsimd.memset(v_sc1[:], 0)
+        wa_first = laid("wa_first", [P, PACK * H], F32, 11264)
+        hw_rows = kept("hw_rows", [P, P], F32)
+        nc.vector.memset(hw_rows[:], 0.0)
+
+        wb_w = laid("wb_w", [P, PACK, PASSES, P // 2], I32, 9216)
+        nc.gpsimd.tensor_copy(
+            wb_w[:].rearrange("p t a (b w) -> p t (a b) w", w=4),
+            wb_raw[:].rearrange("p a (b t w) -> p t (a b) w", t=PACK, w=4),
+        )
+
+        table_at = (0, 19456)
+        tab_w = [laid(f"tab_w{a}", [P, T], I32, table_at[a]) for a in range(PASSES)]
         nc.sync.dma_start(tab_w[0][:], tab_words[0].rearrange("p c i -> p (c i)").bitcast(I32))
         wb_sc_hbm = wb_scales.bitcast(I32).rearrange("a r c -> r a c")
         for q in range(QUADS):
             nc.sync.dma_start(wb_sc_raw[32 * q : 32 * q + 4, :, :], wb_sc_hbm[4 * q : 4 * q + 4])
         nc.sync.dma_start(tab_w[1][:], tab_words[1].rearrange("p c i -> p (c i)").bitcast(I32))
+        wa_hbm = wa.rearrange("(a p j) c -> a p (j c)", a=PASSES, j=PACK)
+        nc.sync.dma_start(wa_first[:, :H], wa_hbm[0, :, :H])
 
         nc.scalar.dma_start(
             hw_rows[0:PACK, :].rearrange("t (b i) -> t b i", i=BLOCK_ROWS),
@@ -84,8 +114,8 @@ def tile_list_campaign_interaction_logits_kernel(
         hw_t = kept("hw_t", [P, PACK], F32)
         minus_hw = kept("minus_hw", [P, PACK], F32)
 
-        inv_root = kept("inv_root", [P, PACK], F32)
-        nc.scalar.activation(inv_root[:], hw_turned[:, 0:PACK], ACT.Abs_reciprocal_sqrt)
+        inv_root = wa_first[:, H : H + PACK]
+        nc.scalar.activation(inv_root, hw_turned[:, 0:PACK], ACT.Abs_reciprocal_sqrt)
         nc.scalar.copy(hw_t[:], hw_turned[:, 0:PACK])
         nc.scalar.activation(minus_hw[:], hw_turned[:, 0:PACK], ACT.Copy, scale=-1.0)
 
@@ -94,7 +124,7 @@ def tile_list_campaign_interaction_logits_kernel(
                 nc.scalar.activation(prod[:, t : t + 1], x[:, t : t + 1], ACT.Copy, scale=y[:, t : t + 1], bias=bias)
 
         minus_half_inv = kept("minus_half_inv", [P, PACK], F32)
-        nc.scalar.activation(minus_half_inv[:], inv_root[:], ACT.Copy, scale=-0.5)
+        nc.scalar.activation(minus_half_inv[:], inv_root, ACT.Copy, scale=-0.5)
         rough_root = kept("rough_root", [P, PACK], F32)
         times(rough_root, hw_t, inv_root)
         correction = kept("correction", [P, PACK], F32)
@@ -111,7 +141,7 @@ def tile_list_campaign_interaction_logits_kernel(
         v_sc = [v_sc0[:], v_sc1[:].bitcast(U8)]
 
         def load_g(u):
-            rows = reused(f"g_tab{u}", [P, T], F32, f"table{u}")
+            rows = laid(f"g_tab{u}", [P, T], F32, (table_at[1], 11264)[u])
             nc.sync.dma_start(rows[:], gT[u * P : (u + 1) * P, :])
             return rows
 
@@ -126,34 +156,26 @@ def tile_list_campaign_interaction_logits_kernel(
 
         v_parts = [kept("v_first", [P, QUART], U32)]
 
-        wb_w = kept("wb_w", [P, PACK, PASSES, P // 2], I32)
-        nc.gpsimd.tensor_copy(
-            wb_w[:].rearrange("p t a (b w) -> p t (a b) w", w=4),
-            wb_raw[:].rearrange("p a (b t w) -> p t (a b) w", t=PACK, w=4),
-        )
-        weights = reused("weights", [P, PASSES * PACK * H + PACK * N], F32, "weights")
-        wa_raw = weights[:, : PASSES * PACK * H].rearrange("p (a j c) -> p a j c", a=PASSES, j=PACK)
-        for a in range(PASSES):
-            nc.sync.dma_start(
-                wa_raw[:, a], wa[a * P * PACK : (a + 1) * P * PACK, :].rearrange("(p j) c -> p j c", j=PACK)
-            )
-        wo_raw = weights[:, PASSES * PACK * H :].rearrange("p (t n) -> p t n", t=PACK)
-        wo_hbm = wo.rearrange("(b t i) n -> t b i n", t=PACK, i=BLOCK_ROWS)
-        for t in range(PACK):
-            nc.sync.dma_start(wo_raw[:, t, :], wo_hbm[t])
-        gather_words(0, 0, QUART)
         wb_sc = kept("wb_sc", [P, PACK, PASSES, P // 4], I32)
         nc.gpsimd.tensor_copy(
             wb_sc[:].rearrange("p t a (b w) -> p t (a b) w", w=2),
             wb_sc_raw[:].rearrange("p a (b t w) -> p t (a b) w", t=PACK, w=2),
         )
+        nc.sync.dma_start(wa_first[:, H:], wa_hbm[0, :, H:])
+        weights = laid("weights", [P, PACK * (H + N)], F32, 28160)
+        nc.sync.dma_start(weights[:, : PACK * H], wa_hbm[1])
+        wa_raw = [rows.rearrange("p (j c) -> p j c", j=PACK) for rows in (wa_first[:], weights[:, : PACK * H])]
+        wo_raw = weights[:, PACK * H :].rearrange("p (t n) -> p t n", t=PACK)
+        wo_hbm = wo.rearrange("(b t i) n -> t b i n", t=PACK, i=BLOCK_ROWS)
+        for t in range(PACK):
+            nc.sync.dma_start(wo_raw[:, t, :], wo_hbm[t])
+        gather_words(0, 0, QUART)
         v_parts.append(kept("v_rest", [P, 2 * S - QUART], U32))
         gather_words(0, QUART, QUART)
         gather_words(0, HALF, HALF)
-        g_tab = [load_g(0)]
         for first, width in ((0, QUART), (QUART, QUART), (HALF, HALF)):
             gather_words(1, first, width)
-        g_tab.append(load_g(1))
+        g_tab = [load_g(0)]
 
         hw_b = [kept(f"hw_b{half}", [P, PACK, HALF], F32) for half in range(2)]
 
@@ -186,7 +208,7 @@ def tile_list_campaign_interaction_logits_kernel(
         def round_wa(a, first, count):
             wa_bf[a, first] = kept(f"wa_bf{a}{first}", [P, count, P, PACK], BF16)
             runs = BLOCK_ROWS // RUN
-            src = wa_raw[:, a].rearrange("p j (b t c i) -> p t b c j i", t=PACK, c=runs, i=RUN)
+            src = wa_raw[a].rearrange("p j (b t c i) -> p t b c j i", t=PACK, c=runs, i=RUN)
             dst = wa_bf[a, first][:].rearrange("p t (b c i) j -> p t b c j i", c=runs, i=RUN)
             for t in range(count):
                 nc.vector.tensor_copy(dst[:, t], src[:, first + t])
@@ -207,6 +229,7 @@ def tile_list_campaign_interaction_logits_kernel(
             round_wa(0, first, 2)
         for first in (0, 2):
             quantize_wa(0, first, 2)
+        g_tab.append(load_g(1))
         round_wa(1, 0, 1)
         for t in range(1, PACK):
             round_wa(1, t, 1)

from contextlib import ExitStack

import concourse.mybir as mybir

K, H, N, T, S = 1024, 512, 256, 2048, 1024
FLOPS = 2 * K * H * S * 2 + 2 * H * N * S

F32 = mybir.dt.float32
BF16 = mybir.dt.bfloat16
I32 = mybir.dt.int32
U32 = mybir.dt.uint32
U16 = mybir.dt.uint16
U8 = mybir.dt.uint8
FP8X4 = mybir.dt.float8_e4m3fn_x4
FP4X4 = mybir.dt.float4_e2m1fn_x4
ALU = mybir.AluOpType
ACT = mybir.ActivationFunctionType

P = 128
PACK = 4
PASSES = K // (P * PACK)
BLOCK_ROWS = 8
QUADS = 4
LIST_ROWS = 16
HALF = S // 2
QUART = S // 4
RUN = 2
LAST = 64


def tile_list_campaign_interaction_logits_kernel(
    tc, tab_words, tab_scales, offs, gT, wa, wb_words, wb_scales, hw, wo, out
):
    nc = tc.nc
    with ExitStack() as ctx:
        keep = ctx.enter_context(tc.tile_pool(name="keep", bufs=1))
        shared = ctx.enter_context(tc.tile_pool(name="shared", bufs=1))
        placed = ctx.enter_context(tc.tile_pool(name="placed", bufs=1))
        psum = ctx.enter_context(tc.psum_pool(name="psum", bufs=1))

        def kept(name, shape, dtype):
            return keep.tile(shape, dtype, name=name, align_bytes=64)

        def reused(name, shape, dtype, buffer):
            return shared.tile(shape, dtype, name=name, tag=buffer, align_bytes=64)

        def laid(name, shape, dtype, offset):
            return placed.tile(shape, dtype, name=name, align_bytes=64, offset=offset)

        offsets = keep.tile([P, S // LIST_ROWS], U16, name="offsets")
        nc.sync.dma_start(offsets[:], offs)

        tab_sc = kept("tab_sc", [P, T // 4], I32)
        nc.gpsimd.memset(tab_sc[:], 0)

        wb_raw = kept("wb_raw", [P, PASSES, H // 2], I32)
        nc.sync.dma_start(wb_raw[:], wb_words.bitcast(I32).rearrange("a p c -> p a c"))

        tab_rows = tab_scales.bitcast(I32).rearrange("a r c -> (a r) c")
        nc.sync.dma_start(tab_sc[0:32, :], tab_rows)
        for q in range(1, QUADS):
            nc.sync.dma_start(tab_sc[32 * q : 32 * q + 4, :], tab_rows[4 * q : 4 * q + 4, :])

        identity = kept("identity", [P, P], F32)

        def cut_identity(ones, first):
            width = ones.shape[1]
            nc.gpsimd.affine_select(
                out=identity[:, first : first + width],
                in_=ones,
                pattern=[[-1, width]],
                compare_op=ALU.is_equal,
                fill=0.0,
                base=-first,
                channel_multiplier=1,
            )

        ones_left = laid("ones_left", [P, 4896], F32, 8128)
        nc.vector.memset(ones_left[:, : P // 2], 1.0)
        cut_identity(ones_left[:, : P // 2], 0)
        wb_sc_raw = laid("wb_sc_raw", [P, PASSES, H // 4], I32, 27648)
        nc.gpsimd.memset(wb_sc_raw[:], 0)
        ones_right = laid("ones_right", [P, 2592], F32, 9152)
        nc.gpsimd.memset(ones_right[:, : P // 2], 1.0)
        cut_identity(ones_right[:, : P // 2], P // 2)
        v_sc1 = laid("v_sc1", [P, S // 4], I32, 8192)
        nc.gpsimd.memset(v_sc1[:], 0)
        wa_first = laid("wa_first", [P, PACK * H], F32, 11264)
        hw_rows = kept("hw_rows", [P, P], F32)
        nc.vector.memset(hw_rows[:], 0.0)

        wb_w = laid("wb_w", [P, PACK, PASSES, P // 2], I32, 9216)
        nc.gpsimd.tensor_copy(
            wb_w[:].rearrange("p t a (b w) -> p t (a b) w", w=4),
            wb_raw[:].rearrange("p a (b t w) -> p t (a b) w", t=PACK, w=4),
        )

        table_at = (0, 19456)
        tab_w = [laid(f"tab_w{a}", [P, T], I32, table_at[a]) for a in range(PASSES)]
        nc.sync.dma_start(tab_w[0][:], tab_words[0].rearrange("p c i -> p (c i)").bitcast(I32))
        wb_sc_hbm = wb_scales.bitcast(I32).rearrange("a r c -> r a c")
        for q in range(QUADS):
            nc.sync.dma_start(wb_sc_raw[32 * q : 32 * q + 4, :, :], wb_sc_hbm[4 * q : 4 * q + 4])
        nc.sync.dma_start(tab_w[1][:], tab_words[1].rearrange("p c i -> p (c i)").bitcast(I32))
        wa_hbm = wa.rearrange("(a p j) c -> a p (j c)", a=PASSES, j=PACK)
        nc.sync.dma_start(wa_first[:, :H], wa_hbm[0, :, :H])

        nc.scalar.dma_start(
            hw_rows[0:PACK, :].rearrange("t (b i) -> t b i", i=BLOCK_ROWS),
            hw.rearrange("(b t i) -> t b i", t=PACK, i=BLOCK_ROWS),
        )
        hw_turned = psum.tile([P, P], F32, name="hw_turned", tag="bank7")
        nc.tensor.transpose(hw_turned[:], hw_rows[:], identity[:])
        hw_t = kept("hw_t", [P, PACK], F32)
        minus_hw = kept("minus_hw", [P, PACK], F32)

        inv_root = wa_first[:, H : H + PACK]
        nc.scalar.activation(inv_root, hw_turned[:, 0:PACK], ACT.Abs_reciprocal_sqrt)
        nc.scalar.copy(hw_t[:], hw_turned[:, 0:PACK])
        nc.scalar.activation(minus_hw[:], hw_turned[:, 0:PACK], ACT.Copy, scale=-1.0)

        def times(prod, x, y, bias=0.0):
            for t in range(PACK):
                nc.scalar.activation(prod[:, t : t + 1], x[:, t : t + 1], ACT.Copy, scale=y[:, t : t + 1], bias=bias)

        minus_half_inv = kept("minus_half_inv", [P, PACK], F32)
        nc.scalar.activation(minus_half_inv[:], inv_root, ACT.Copy, scale=-0.5)
        rough_root = kept("rough_root", [P, PACK], F32)
        times(rough_root, hw_t, inv_root)
        correction = kept("correction", [P, PACK], F32)
        times(correction, rough_root, minus_half_inv, bias=1.5)
        roots = [reused(f"root{quart}", [P, PACK], F32, f"root{quart}") for quart in range(4)]
        times(roots[0], rough_root, correction)
        for quart in range(1, 4):
            nc.scalar.copy(roots[quart][:], roots[0][:])

        v_sc0 = kept("v_sc0", [P, S], U8)
        nc.vector.tensor_copy(v_sc0[:], tab_sc[:].bitcast(U8).indirect(offsets[:]))
        for q in range(QUADS):
            nc.sync.dma_start(v_sc1[32 * q : 32 * q + 4, :], v_sc0[16 + 4 * q : 20 + 4 * q, :].bitcast(I32))
        v_sc = [v_sc0[:], v_sc1[:].bitcast(U8)]

        def load_g(u):
            rows = laid(f"g_tab{u}", [P, T], F32, (table_at[1], 11264)[u])
            nc.sync.dma_start(rows[:], gT[u * P : (u + 1) * P, :])
            return rows

        def gather_words(a, first, width):
            entries = slice(first // LIST_ROWS, (first + width) // LIST_ROWS)
            nc.vector.tensor_copy(words_of(a, first, width), tab_w[a][:].bitcast(U32).indirect(offsets[:, entries]))

        def words_of(a, first, width):
            if a * S + first < QUART:
                return v_parts[0][:, first : first + width]
            return v_parts[1][:, a * S + first - QUART : a * S + first - QUART + width]

        v_parts = [kept("v_first", [P, QUART], U32)]

        wb_sc = kept("wb_sc", [P, PACK, PASSES, P // 4], I32)
        nc.gpsimd.tensor_copy(
            wb_sc[:].rearrange("p t a (b w) -> p t (a b) w", w=2),
            wb_sc_raw[:].rearrange("p a (b t w) -> p t (a b) w", t=PACK, w=2),
        )
        nc.sync.dma_start(wa_first[:, H:], wa_hbm[0, :, H:])
        weights = laid("weights", [P, PACK * (H + N)], F32, 28160)
        nc.sync.dma_start(weights[:, : PACK * H], wa_hbm[1])
        wa_raw = [rows.rearrange("p (j c) -> p j c", j=PACK) for rows in (wa_first[:], weights[:, : PACK * H])]
        wo_raw = weights[:, PACK * H :].rearrange("p (t n) -> p t n", t=PACK)
        wo_hbm = wo.rearrange("(b t i) n -> t b i n", t=PACK, i=BLOCK_ROWS)
        for t in range(PACK):
            nc.sync.dma_start(wo_raw[:, t, :], wo_hbm[t])
        gather_words(0, 0, QUART)
        v_parts.append(kept("v_rest", [P, 2 * S - QUART], U32))
        gather_words(0, QUART, QUART)
        gather_words(0, HALF, HALF)
        for first, width in ((0, QUART), (QUART, QUART), (HALF, HALF)):
            gather_words(1, first, width)
        g_tab = [load_g(0)]

        hw_b = [kept(f"hw_b{half}", [P, PACK, HALF], F32) for half in range(2)]

        def weighted_b(first, width, step, bank):
            half, lo = first // HALF, first % HALF
            groups = [psum.tile([P, width], F32, name=f"b{first}_{t}", tag=f"bank{bank + t}") for t in range(PACK)]
            for t in range(PACK):
                for a in range(PASSES):
                    for c in range(0, width, step):
                        nc.tensor.matmul_mx(
                            out=groups[t][:, c : c + step],
                            lhsT=wb_w[:, t, a, :].bitcast(FP4X4),
                            lhsT_scale=wb_sc[:, t, a, :].bitcast(U8),
                            rhs=words_of(a, first + c, step).bitcast(FP8X4),
                            rhs_scale=v_sc[a][:, first + c : first + c + step],
                            start=(a == 0 and c == 0),
                            stop=(a == PASSES - 1 and c == width - step),
                        )
            for t in range(PACK):
                nc.scalar.activation(hw_b[half][:, t, lo : lo + width], groups[t][:], ACT.Copy, scale=minus_hw[:, t : t + 1])

        weighted_b(0, QUART, QUART, 0)
        weighted_b(QUART, QUART, QUART, 4)
        weighted_b(HALF, HALF, HALF, 0)

        wa_w = {}
        wa_sc = {}
        wa_bf = {}

        def round_wa(a, first, count):
            wa_bf[a, first] = kept(f"wa_bf{a}{first}", [P, count, P, PACK], BF16)
            runs = BLOCK_ROWS // RUN
            src = wa_raw[a].rearrange("p j (b t c i) -> p t b c j i", t=PACK, c=runs, i=RUN)
            dst = wa_bf[a, first][:].rearrange("p t (b c i) j -> p t b c j i", c=runs, i=RUN)
            for t in range(count):
                nc.vector.tensor_copy(dst[:, t], src[:, first + t])

        def quantize_wa(a, first, count):
            codes = kept(f"wa_w{a}{first}", [P, count, P], U32)
            scales = kept(f"wa_sc{a}{first}", [P, count, P], U8)
            nc.vector.quantize_mx(
                out=codes[:].rearrange("p t m -> p (t m)").bitcast(FP8X4),
                scales=scales[:].rearrange("p t m -> p (t m)"),
                in_=wa_bf[a, first][:].rearrange("p t m j -> p (t m j)"),
            )
            for t in range(count):
                wa_w[a, first + t] = codes[:, t, :]
                wa_sc[a, first + t] = scales[:, t, :]

        for first in (0, 2):
            round_wa(0, first, 2)
        for first in (0, 2):
            quantize_wa(0, first, 2)
        g_tab.append(load_g(1))
        round_wa(1, 0, 1)
        for t in range(1, PACK):
            round_wa(1, t, 1)
            quantize_wa(1, t - 1, 1)
        quantize_wa(1, PACK - 1, 1)

        a_groups = {}

        def product_a(quart, slots):
            cols = slice(quart * QUART, (quart + 1) * QUART)
            if quart == 1:
                for t in range(2):
                    both = psum.tile([P, 2, QUART], F32, name=f"a{quart}{t}", tag=f"bank{t}")
                    a_groups[quart, t], a_groups[quart, PACK - 1 - t] = both[:, 0, :], both[:, 1, :]
            for t in slots:
                if quart != 1:
                    a_groups[quart, t] = psum.tile([P, QUART], F32, name=f"a{quart}{t}", tag=f"bank{4 * (1 - quart % 2) + t}")[:]
                order = (0, 1) if quart == 0 else (1, 0)
                for a in order:
                    nc.tensor.matmul_mx(
                        out=a_groups[quart, t],
                        lhsT=wa_w[a, t].bitcast(FP8X4),
                        lhsT_scale=wa_sc[a, t],
                        rhs=words_of(a, quart * QUART, QUART).bitcast(FP8X4),
                        rhs_scale=v_sc[a][:, cols],
                        start=(a == order[0]),
                        stop=(a == order[-1]),
                    )

        hw_a2 = [kept(f"hw_a2_{quart}", [P, PACK, QUART], F32) for quart in range(4)]

        def square_a(quart, slots):
            for t in slots:
                nc.scalar.activation(hw_a2[quart][:, t, :], a_groups[quart, t], ACT.Square, scale=roots[quart][:, t : t + 1])

        def side_by_side(ap):
            return ap.rearrange("p (c i) t -> p c t i", i=RUN)

        def by_slot(ap):
            return ap.rearrange("p t (c i) -> p c t i", i=RUN)

        wo_bf = [kept(f"wo_bf{u}", [P, P, PACK], BF16) for u in range(2)]
        wo_w = [kept(f"wo_w{u}", [P, P], U32) for u in range(2)]
        wo_sc = [kept(f"wo_sc{u}", [P, P], U8) for u in range(2)]
        for u in range(2):
            nc.vector.tensor_copy(side_by_side(wo_bf[u][:]), by_slot(wo_raw[:, :, u * P : (u + 1) * P]))
        for u in range(2):
            nc.vector.quantize_mx(
                out=wo_w[u][:].bitcast(FP8X4), scales=wo_sc[u][:], in_=wo_bf[u][:].rearrange("p n t -> p (n t)")
            )
        for quart in range(4):
            product_a(quart, (1, 2, 0, 3) if quart == 1 else range(PACK))
            square_a(quart, (1, 2, 0, 3) if quart == 1 else range(PACK))

        h_bf = {}
        h_w = {}
        h_sc = [kept(f"h_sc{quart}", [P, QUART], U8) for quart in range(4)]
        half_y = {}
        out_view = out.rearrange("(u p) j -> p u j", p=P)

        def subtract(quart, width=QUART):
            half, lo = quart // 2, (quart % 2) * QUART
            h_bf[quart] = reused(f"h_bf{quart}", [P, QUART, PACK], BF16, f"rounded{quart}")
            nc.vector.tensor_tensor(
                side_by_side(h_bf[quart][:, :width]),
                by_slot(hw_a2[quart][:, :, :width]),
                by_slot(hw_b[half][:, :, lo : lo + width]),
                ALU.add,
            )

        def quantize_h(quart, buffer):
            h_w[quart] = reused(f"h_w{quart}", [P, QUART], U32, buffer)
            nc.vector.quantize_mx(
                out=h_w[quart][:].bitcast(FP8X4),
                scales=h_sc[quart][:],
                in_=h_bf[quart][:].rearrange("p j t -> p (j t)"),
            )

        def subtract_by_transposes(quart, first):
            half, lo = quart // 2, (quart % 2) * QUART + first
            sums = psum.tile([P, PACK, P], F32, name="h_turned", tag="bank7")
            for t in range(PACK):
                minus_b = hw_b[half][:, t, lo : lo + P]
                nc.tensor.matmul(sums[:, t, :], minus_b, identity[:], start=(t == 0), stop=False, is_transpose=True)
            for t in range(PACK):
                square = hw_a2[quart][:, t, first : first + P]
                nc.tensor.matmul(sums[:, t, :], square, identity[:], start=False, stop=(t == PACK - 1), is_transpose=True)
            pairs = reused("h_pairs", [P, 2, P, 2], BF16, "pairs")
            nc.scalar.copy(pairs[:], sums[:].rearrange("j (u e) p -> j u p e", e=2))
            words = psum.tile([P, 2, P], F32, name="h_words", tag="bank1")
            for u in range(2):
                nc.tensor.transpose(words[:, u, :], pairs[:, u].rearrange("j p e -> j (p e)").bitcast(F32), identity[:])
            return words

        def copy_words(quart, first, words):
            side = h_bf[quart][:, first : first + P].rearrange("p j t -> p (j t)").bitcast(F32)
            nc.scalar.copy(side.rearrange("p (j u) -> p j u", u=2), words[:].rearrange("p u j -> p j u"))

        def product_y(quart):
            y = psum.tile([P, 2, QUART], F32, name=f"y{quart}", tag=f"bank{(4, 5, 6, 0)[quart]}")
            for u in range(2):
                nc.tensor.matmul_mx(
                    out=y[:, u, :],
                    lhsT=wo_w[u][:].bitcast(FP8X4),
                    lhsT_scale=wo_sc[u][:],
                    rhs=h_w[quart][:].bitcast(FP8X4),
                    rhs_scale=h_sc[quart][:],
                    start=True,
                    stop=True,
                )
            return y

        def halve(quart, y, dst, groups=slice(0, 2)):
            nc.scalar.activation(dst, y[:, groups, :], ACT.Copy, scale=0.5)
            for u in range(groups.start, groups.stop):
                half_y[quart, u] = dst[:, u - groups.start, :]

        def finish(quart, buffer):
            cols = slice(quart * QUART, (quart + 1) * QUART)
            result = reused(f"result{quart}", [P, 2, QUART], F32, buffer)
            pieces = [(0, 0, QUART), (1, 0, QUART)]
            if quart == 3:
                pieces = [(0, 0, QUART), (1, 0, QUART - LAST), (1, QUART - LAST, QUART)]
            for u, lo, hi in pieces:
                first, last = quart * QUART + lo, quart * QUART + hi
                entries = offsets[:, first // LIST_ROWS : last // LIST_ROWS]
                nc.vector.tensor_tensor(
                    result[:, u, lo:hi], g_tab[u][:].indirect(entries), half_y[quart, u][:, lo:hi], ALU.add
                )
                if quart == 3:
                    nc.sync.dma_start(out_view[:, u, first:last], result[:, u, lo:hi])
            if quart < 3:
                nc.sync.dma_start(out_view[:, :, cols], result[:])

        subtract(0)
        subtract(1)
        quantize_h(0, "root1")
        halve(0, product_y(0), kept("half_y0", [P, 2, QUART], F32)[:])
        subtract(2)
        quantize_h(1, "root2")
        subtract(3, P)
        quantize_h(2, "root3")
        words = subtract_by_transposes(3, P)
        y1 = product_y(1)
        halve(1, y1, kept("half_y10", [P, 1, QUART], F32)[:], slice(0, 1))
        copy_words(3, P, words)
        quantize_h(3, "codes3")
        late = reused("half_y_late", [P, 3, QUART], F32, "pairs")
        halve(1, y1, late[:, 0:1, :], slice(1, 2))
        halve(2, product_y(2), late[:, 1:3, :])
        y3 = product_y(3)
        for u in range(2):
            halve(3, y3, kept(f"half_y3{u}", [P, 1, QUART], F32)[:], slice(u, u + 1))
        finish(0, "result0")
        finish(1, "result1")
        finish(2, "result2")
        finish(3, "result3")
